import numpy as np
import ml_dtypes


def mxq(x, axis, fmt="e4m3"):
    dtype, down = {"e4m3": (ml_dtypes.float8_e4m3fn, 7), "e5m2": (ml_dtypes.float8_e5m2, 14)}[fmt]
    v = np.moveaxis(np.asarray(x, np.float32).astype(ml_dtypes.bfloat16).astype(np.float64), axis, -1)
    blocks = v.reshape(v.shape[:-1] + (-1, 32))
    amax = np.abs(blocks).max(-1, keepdims=True)
    byte = np.maximum(np.where(amax > 0, np.frexp(amax)[1] - 1 + 127, 0) - down, 1)
    scale = np.exp2(byte - 127.0)
    codes = (blocks / scale).astype(np.float32).astype(dtype).astype(np.float64)
    return np.moveaxis((codes * scale).reshape(v.shape), -1, axis)


WIDE = False


def mx_kscale(k):
    if not WIDE:
        return np.ones(k)
    levels = np.array([10, -10, 5, -5, 0])
    if k % 512:
        return np.exp2(np.random.permutation(np.resize(levels, k // 32))).repeat(32)
    a = np.empty((k // 512, 16))
    for p in range(k // 512):
        a[p, :8] = np.random.permutation(np.resize(levels, 8))
        for g in range(8):
            far = levels[np.abs(levels - a[p, g]) >= 10]
            a[p, g + 8] = far[np.random.randint(len(far))]
    return np.exp2(a.ravel()).repeat(32)


def f64(x):
    return np.asarray(x).astype(np.float64)


def striped(idx):
    return np.tile(idx.reshape(-1, 16).T, (8, 1)).astype(np.uint16)


def unstriped(offs):
    return offs[:16].T.reshape(-1).astype(np.int64)


E2M1 = np.array([0.0, 0.5, 1.0, 1.5, 2.0, 3.0, 4.0, 6.0, -0.0, -0.5, -1.0, -1.5, -2.0, -3.0, -4.0, -6.0])


def pack_weight(w, fmt):
    k, n = w.shape
    w = f64(np.asarray(w, np.float32).astype(ml_dtypes.bfloat16)).reshape(k // 32, 32, n)
    amax = np.abs(w).max(1)
    if fmt == "e4m3":
        byte = np.frexp(amax)[1] - 1 + 127 - 7
    else:
        mant, ex = np.frexp(amax / 6.0)
        byte = np.where(mant > 0.5, ex, ex - 1) + 127
    byte = np.clip(np.where(amax > 0, byte, 1), 1, 254)
    scaled = (w * np.exp2(127.0 - byte)[:, None, :]).reshape(k, n).astype(np.float32)
    by_word = np.ascontiguousarray(scaled.reshape(k // 512, 128, 4, n).transpose(0, 1, 3, 2))
    if fmt == "e4m3":
        words = by_word.astype(ml_dtypes.float8_e4m3fn).view(np.uint8)
    else:
        c = by_word.astype(ml_dtypes.float4_e2m1fn).view(np.uint8) & 0xF
        words = (c[..., 0::2] | (c[..., 1::2] << 4)).reshape(k // 512, 128, 2 * n)
    return np.ascontiguousarray(words), np.ascontiguousarray(byte.astype(np.uint8).reshape(k // 512, 16, n))


def unpack_weight(words, scales, fmt):
    g, _, n = scales.shape
    words = np.ascontiguousarray(words).reshape(g, 128, n, -1)
    if fmt == "e4m3":
        vals = words.view(ml_dtypes.float8_e4m3fn).astype(np.float64)
    else:
        nib = np.empty((g, 128, n, 4), np.uint8)
        nib[..., 0::2] = words & 0xF
        nib[..., 1::2] = words >> 4
        vals = E2M1[nib]
    vals = vals * np.repeat(np.exp2(scales.astype(np.float64) - 127.0), 8, axis=1)[..., None]
    return vals.transpose(0, 1, 3, 2).reshape(g * 512, n)


def gelu(v):
    return 0.5 * v * (1.0 + np.tanh(np.sqrt(2.0 / np.pi) * (v + 0.044715 * v**3)))


K, T, S, H, G, N = 1024, 4096, 1024, 1024, 512, 512

def setup_inputs():
    n = np.random.standard_normal
    s = mx_kscale(K)[:, None]
    u = mx_kscale(H)[:, None]
    x = mx_kscale(G)[:, None]
    tab_words, tab_scales = pack_weight(n((K, T)) * s, "e2m1")
    w2_words, w2_scales = pack_weight(1.5 * n((K, G)) / np.sqrt(K) / s, "e4m3")
    w3_words, w3_scales = pack_weight(n((H, N)) / np.sqrt(H) / u, "e2m1")
    return {
        "tab_words": tab_words, "tab_scales": tab_scales,
        "offs": striped(np.random.permutation(T)[:S]),
        "offs2": striped(np.random.permutation(T)[:S]),
        "w1": (n((K, H)) / np.sqrt(K) / s).astype(np.float32),
        "gain1": (np.exp(0.3 * n(H)) * u[:, 0]).astype(np.float32),
        "w2_words": w2_words, "w2_scales": w2_scales,
        "bias2": (0.5 * n(G)).astype(np.float32),
        "gain2": (np.exp(0.3 * n(G)) * x[:, 0]).astype(np.float32),
        "w3_words": w3_words, "w3_scales": w3_scales,
        "w4": (1.5 * n((G, N)) / np.sqrt(G) / x).astype(np.float32),
    }

def reference(tab_words, tab_scales, offs, offs2, w1, gain1, w2_words, w2_scales, bias2, gain2, w3_words, w3_scales, w4):
    TW = unpack_weight(tab_words, tab_scales, "e2m1")
    v = TW[:, unstriped(offs)]
    v2 = TW[:, unstriped(offs2)]
    w2 = unpack_weight(w2_words, w2_scales, "e4m3")
    w3 = unpack_weight(w3_words, w3_scales, "e2m1")
    h = f64(gain1)[:, None] * np.tanh(mxq(f64(w1), 0, "e4m3").T @ v)
    b = (w2.T @ v2) + f64(bias2)[:, None]
    d = f64(gain2)[:, None] * (1.0 / (1.0 + np.exp(-b)))
    y = w3.T @ mxq(h, 0, "e4m3") + mxq(f64(w4), 0, "e4m3").T @ mxq(d, 0, "e4m3")
    return 0.5 * y * (1.0 + np.tanh(np.sqrt(2.0 / np.pi) * (y + 0.044715 * y ** 3)))

@@ -1,0 +1,275 @@
+from contextlib import ExitStack
+
+import concourse.mybir as mybir
+
+K, T, S, H, G, N = 1024, 4096, 1024, 1024, 512, 512
+FLOPS = 2 * S * (K * H + K * G + H * N + G * N)
+
+F32 = mybir.dt.float32
+BF16 = mybir.dt.bfloat16
+I32 = mybir.dt.int32
+U32 = mybir.dt.uint32
+U16 = mybir.dt.uint16
+U8 = mybir.dt.uint8
+FP8X4 = mybir.dt.float8_e4m3fn_x4
+FP4X4 = mybir.dt.float4_e2m1fn_x4
+ACT = mybir.ActivationFunctionType
+MULT = mybir.AluOpType.mult
+
+P = 128
+PACK = 4
+KP = P * PACK
+QUADS = 4
+QUAD = 32
+SROWS = 4
+SHIFTED = 112
+CH = 128
+HALF = 512
+
+
+def tile_list_unfollow_forecast_features_kernel(
+    tc, tab_words, tab_scales, offs, offs2, w1, gain1, w2_words, w2_scales, bias2, gain2, w3_words, w3_scales, w4, out
+):
+    nc = tc.nc
+    passes = K // KP
+    blocks = H // KP
+    chunks = S // CH
+    halves = S // HALF
+
+    with ExitStack() as ctx:
+        keep = ctx.enter_context(tc.tile_pool(name="keep", bufs=1))
+        stage = ctx.enter_context(tc.tile_pool(name="stage", bufs=2))
+        ps1 = ctx.enter_context(tc.psum_pool(name="ps1", bufs=5))
+        ps2 = ctx.enter_context(tc.psum_pool(name="ps2", bufs=3))
+
+        def sb(name, shape, dtype, tag=None):
+            return keep.tile(shape, dtype, name=name, tag=tag or name, align_bytes=64)
+
+        list1 = keep.tile([P, S // 16], U16, name="list1")
+        list2 = keep.tile([P, S // 16], U16, name="list2")
+        wwin = [sb("wwin%d" % a, [P, T], U16) for a in range(passes)]
+        g1 = sb("g1", [P, blocks, PACK], F32)
+        g2 = sb("g2", [P, PACK], F32)
+        b2 = sb("b2", [P, PACK], F32)
+
+        def load_tab(a, c0, c1):
+            nc.sync.dma_start(wwin[a][:, c0:c1].bitcast(I32), tab_words[a][:, 2 * c0 : 2 * c1].bitcast(I32))
+
+        nc.sync.dma_start(list1[:], offs)
+        for f in range(4):
+            load_tab(0, T // 4 * f, T // 4 * (f + 1))
+        nc.sync.dma_start(g1[:], gain1.rearrange("(b p t) -> p b t", b=blocks, t=PACK))
+        nc.sync.dma_start(b2[:], bias2.rearrange("(p t) -> p t", t=PACK))
+        nc.sync.dma_start(g2[:], gain2.rearrange("(p t) -> p t", t=PACK))
+
+        swin = sb("swin", [P, T], U8)
+        nc.vector.memset(swin[:].bitcast(I32), 0)
+        for q in range(QUADS):
+            nc.sync.dma_start(
+                swin[QUAD * q : QUAD * q + passes * SROWS, :].bitcast(I32),
+                tab_scales[:, SROWS * q : SROWS * (q + 1), :].bitcast(I32),
+            )
+
+        warm_in = sb("warm_in", [P, 1], F32)
+        warm_out = sb("warm_out", [P, 1], F32)
+        nc.gpsimd.memset(warm_in[:], 0.0)
+        nc.scalar.activation(warm_out[:], warm_in[:], ACT.Sigmoid)
+
+        def zeroed(name, shape, tag=None):
+            t = sb(name, shape, U8, tag)
+            nc.gpsimd.memset(t[:].bitcast(I32), 0)
+            return t
+
+        def load_scale_rows(queue, plane, scales):
+            for q in range(QUADS):
+                queue.dma_start(
+                    plane[QUAD * q : QUAD * q + SROWS].bitcast(I32),
+                    scales[:, SROWS * q : SROWS * (q + 1), :].rearrange("a r c -> r a c").bitcast(I32),
+                )
+
+        s1 = [sb("s1_0", [P, S], U8), zeroed("s1_1", [P, S])]
+        s2 = [sb("s2_0", [P, S], U8), zeroed("s2_1", [P, S])]
+
+        w1_raw = {}
+        w1_codes = {}
+        w1_scales = {}
+
+        def load_w1(a, b):
+            raw = stage.tile([P, PACK, KP], F32, name="raw")
+            nc.sync.dma_start(raw[:], w1[KP * a : KP * (a + 1), KP * b : KP * (b + 1)].rearrange("(p j) c -> p j c", j=PACK))
+            w1_raw[a, b] = raw
+
+        def prep_w1(a, b):
+            grouped = sb("w1bf%d%d" % (a, b), [P, PACK * KP], BF16)
+            nc.scalar.copy(
+                grouped[:].rearrange("p (t m j) -> p m j t", t=PACK, j=PACK),
+                w1_raw[a, b][:].rearrange("p j (m t) -> p m j t", t=PACK),
+            )
+            codes = sb("w1c%d%d" % (a, b), [P, KP], U32)
+            scales = sb("w1s%d%d" % (a, b), [P, KP], U8)
+            nc.vector.quantize_mx(out=codes[:].bitcast(FP8X4), scales=scales[:], in_=grouped[:])
+            w1_codes[a, b] = codes
+            w1_scales[a, b] = scales
+
+        load_w1(0, 0)
+        nc.sync.dma_start(list2[:], offs2)
+        load_w1(1, 0)
+        load_tab(1, 0, T)
+        w2s_raw = zeroed("w2s_raw", [P, passes, G])
+        load_scale_rows(nc.sync, w2s_raw, w2_scales)
+
+        def gather_scales(planes, offsets):
+            nc.vector.tensor_copy(planes[0][:], swin[:].indirect(offsets[:]))
+            nc.sync.dma_start(planes[1][0:SHIFTED, :].bitcast(I32), planes[0][SROWS : SROWS + SHIFTED, :].bitcast(I32))
+
+        v1 = [sb("v1_%d" % a, [P, S], U16) for a in range(passes)]
+        v2 = [sb("v2_%d" % a, [P, S], U16) for a in range(passes)]
+        nc.vector.tensor_copy(v1[0][:], wwin[0][:].indirect(list1[:]))
+        gather_scales(s1, list1)
+        prep_w1(0, 0)
+        gather_scales(s2, list2)
+        load_w1(0, 1)
+        w2_raw = sb("w2_raw", [P, passes, G], I32, "w1bf00")
+        nc.sync.dma_start(w2_raw[:], w2_words.rearrange("a p c i -> p a (c i)").bitcast(I32))
+        prep_w1(1, 0)
+        nc.vector.tensor_copy(v2[0][:], wwin[0][:].indirect(list2[:]))
+        load_w1(1, 1)
+        w4_raw = sb("w4_raw", [P, PACK, N], F32, "w1bf10")
+        nc.sync.dma_start(w4_raw[:], w4.rearrange("(p j) n -> p j n", j=PACK))
+        for f in range(halves):
+            nc.vector.tensor_copy(
+                v1[1][:, HALF * f : HALF * (f + 1)],
+                wwin[1][:].indirect(list1[:, HALF // 16 * f : HALF // 16 * (f + 1)]),
+            )
+        nc.vector.tensor_copy(v2[1][:], wwin[1][:].indirect(list2[:]))
+
+        prep_w1(0, 1)
+        prep_w1(1, 1)
+        w3s = zeroed("w3s", [P, blocks, N], "w1bf01")
+        load_scale_rows(nc.sync, w3s, w3_scales)
+        w3c = sb("w3c", [P, blocks, 2 * N], U8, "w1bf11")
+        nc.sync.dma_start(w3c[:].bitcast(I32), w3_words.rearrange("a p n -> p a n").bitcast(I32))
+
+        h_bf = [sb("hbf%d" % b, [P, PACK * S], BF16) for b in range(blocks)]
+        h_codes = [sb("hc%d" % b, [P, S], U32) for b in range(blocks)]
+        h_scales = [sb("hs%d" % b, [P, S], U8) for b in range(blocks)]
+
+        def h_chunk(b, c, th):
+            cols = slice(CH * c, CH * (c + 1))
+            bank = ps1.tile([P, PACK, CH], F32, name="bank1")
+            for t in range(PACK):
+                for a in range(passes):
+                    nc.tensor.matmul_mx(
+                        out=bank[:, t, :],
+                        lhsT=w1_codes[a, b][:, P * t : P * (t + 1)].bitcast(FP8X4),
+                        lhsT_scale=w1_scales[a, b][:, P * t : P * (t + 1)],
+                        rhs=v1[a][:, cols].bitcast(FP4X4),
+                        rhs_scale=s1[a][:, cols],
+                        start=(a == 0),
+                        stop=(a == passes - 1),
+                    )
+            nc.scalar.activation(th, bank[:].rearrange("p t n -> p n t"), ACT.Tanh)
+            nc.vector.tensor_tensor(
+                h_bf[b][:, PACK * CH * c : PACK * CH * (c + 1)].rearrange("p (n t) -> p n t", t=PACK),
+                th,
+                g1[:, b : b + 1, :].to_broadcast([P, CH, PACK]),
+                MULT,
+            )
+
+        def quantize(codes, scales, values, c0, c1):
+            nc.vector.quantize_mx(
+                out=codes[:, c0:c1].bitcast(FP8X4), scales=scales[:, c0:c1], in_=values[:, PACK * c0 : PACK * c1]
+            )
+
+        per_half = chunks // halves
+        th_first = stage.tile([P, per_half, CH, PACK], F32, name="raw")
+        for c in range(per_half):
+            h_chunk(0, c, th_first[:, c])
+        quantize(h_codes[0], h_scales[0], h_bf[0], 0, HALF)
+
+        w2c = sb("w2c", [P, passes, G], I32)
+        w2s = sb("w2s", [P, passes, G], U8)
+        nc.vector.tensor_copy(
+            w2c[:].rearrange("p a (t m) -> p a m t", t=PACK), w2_raw[:].rearrange("p a (m t) -> p a m t", t=PACK)
+        )
+        nc.vector.tensor_copy(
+            w2s[:].rearrange("p a (t m) -> p a m t", t=PACK), w2s_raw[:].rearrange("p a (m t) -> p a m t", t=PACK)
+        )
+        d_bf = sb("dbf", [P, PACK * S], BF16)
+        d_codes = sb("dc", [P, S], U32)
+        d_scales = sb("ds", [P, S], U8)
+        for f in range(halves):
+            sig = sb("sig%d" % f, [P, PACK, HALF], F32)
+            for t in range(PACK):
+                bank = ps1.tile([P, HALF], F32, name="bank1")
+                for a in range(passes):
+                    nc.tensor.matmul_mx(
+                        out=bank[:],
+                        lhsT=w2c[:, a, P * t : P * (t + 1)].bitcast(FP8X4),
+                        lhsT_scale=w2s[:, a, P * t : P * (t + 1)],
+                        rhs=v2[a][:, HALF * f : HALF * (f + 1)].bitcast(FP4X4),
+                        rhs_scale=s2[a][:, HALF * f : HALF * (f + 1)],
+                        start=(a == 0),
+                        stop=(a == passes - 1),
+                    )
+                nc.scalar.activation(sig[:, t, :], bank[:], ACT.Sigmoid, bias=b2[:, t : t + 1])
+            nc.vector.tensor_tensor(
+                d_bf[:, PACK * HALF * f : PACK * HALF * (f + 1)].rearrange("p (c i t) -> p c t i", i=PACK, t=PACK),
+                sig[:].rearrange("p t (c i) -> p c t i", i=PACK),
+                g2[:].rearrange("p (c t i) -> p c t i", c=1, i=1).to_broadcast([P, HALF // PACK, PACK, PACK]),
+                MULT,
+            )
+            quantize(d_codes, d_scales, d_bf, HALF * f, HALF * (f + 1))
+
+        w4_bf = sb("w4bf", [P, PACK * N], BF16)
+        nc.vector.tensor_copy(
+            w4_bf[:].rearrange("p (c i t) -> p c t i", i=PACK, t=PACK),
+            w4_raw[:].rearrange("p t (c i) -> p c t i", i=PACK),
+        )
+        w4c = sb("w4c", [P, N], U32)
+        w4s = sb("w4s", [P, N], U8)
+        quantize(w4c, w4s, w4_bf, 0, N)
+
+        out_v = out.rearrange("(i p) j -> p i j", p=P)
+
+        def y_chunk(c):
+            cols = slice(CH * c, CH * (c + 1))
+            bank = ps2.tile([P, N // P, CH], F32, name="bank2")
+            for i in range(N // P):
+                rows = slice(P * i, P * (i + 1))
+                nc.tensor.matmul_mx(
+                    out=bank[:, i, :],
+                    lhsT=w4c[:, rows].bitcast(FP8X4),
+                    lhsT_scale=w4s[:, rows],
+                    rhs=d_codes[:, cols].bitcast(FP8X4),
+                    rhs_scale=d_scales[:, cols],
+                    start=(i == 0),
+                    stop=False,
+                )
+            for b in range(blocks):
+                for i in range(N // P):
+                    nc.tensor.matmul_mx(
+                        out=bank[:, i, :],
+                        lhsT=w3c[:, b, 2 * P * i : 2 * P * (i + 1)].bitcast(FP4X4),
+                        lhsT_scale=w3s[:, b, P * i : P * (i + 1)],
+                        rhs=h_codes[b][:, cols].bitcast(FP8X4),
+                        rhs_scale=h_scales[b][:, cols],
+                        start=False,
+                        stop=(b == blocks - 1 and i == N // P - 1),
+                    )
+            res = sb("res%d" % c, [P, N // P, CH], F32)
+            nc.scalar.activation(res[:], bank[:], ACT.Gelu_apprx_tanh)
+            nc.sync.dma_start(out_v[:, :, cols], res[:])
+
+        th_second = stage.tile([P, per_half, CH, PACK], F32, name="raw")
+        for c in range(chunks + 1):
+            if per_half <= c < chunks:
+                h_chunk(0, c, th_second[:, c - per_half])
+            if c > 0:
+                quantize(h_codes[1], h_scales[1], h_bf[1], CH * (c - 1), CH * c)
+            if c < chunks:
+                h_chunk(1, c, sb("th%d" % c, [P, CH, PACK], F32)[:])
+            if per_half <= c < chunks:
+                quantize(h_codes[0], h_scales[0], h_bf[0], CH * c, CH * (c + 1))
+            if c > 0:
+                y_chunk(c - 1)

@@ -22,7 +22,7 @@ KP = P * PACK
 QUADS = 4
 QUAD = 32
 SROWS = 4
-SHIFTED = 112
+SHIFT = 16
 CH = 128
 HALF = 512
 
@@ -64,11 +64,9 @@ def tile_list_unfollow_forecast_features_kernel(
 
         swin = sb("swin", [P, T], U8)
         nc.vector.memset(swin[:].bitcast(I32), 0)
-        for q in range(QUADS):
-            nc.sync.dma_start(
-                swin[QUAD * q : QUAD * q + passes * SROWS, :].bitcast(I32),
-                tab_scales[:, SROWS * q : SROWS * (q + 1), :].bitcast(I32),
-            )
+        scale_rows = tab_scales.rearrange("a (q r) c -> r q a c", r=SROWS)
+        for r in range(SROWS):
+            nc.sync.dma_start(swin[r : P : SHIFT, :].bitcast(I32), scale_rows[r].bitcast(I32))
 
         warm_in = sb("warm_in", [P, 1], F32)
         warm_out = sb("warm_out", [P, 1], F32)
@@ -120,7 +118,7 @@ def tile_list_unfollow_forecast_features_kernel(
 
         def gather_scales(planes, offsets):
             nc.vector.tensor_copy(planes[0][:], swin[:].indirect(offsets[:]))
-            nc.sync.dma_start(planes[1][0:SHIFTED, :].bitcast(I32), planes[0][SROWS : SROWS + SHIFTED, :].bitcast(I32))
+            nc.sync.dma_start(planes[1][0 : P - SHIFT, :].bitcast(I32), planes[0][SHIFT:P, :].bitcast(I32))
 
         v1 = [sb("v1_%d" % a, [P, S], U16) for a in range(passes)]
         v2 = [sb("v2_%d" % a, [P, S], U16) for a in range(passes)]
@@ -258,8 +256,10 @@ def tile_list_unfollow_forecast_features_kernel(
                         stop=(b == blocks - 1 and i == N // P - 1),
                     )
             res = sb("res%d" % c, [P, N // P, CH], F32)
-            nc.scalar.activation(res[:], bank[:], ACT.Gelu_apprx_tanh)
-            nc.sync.dma_start(out_v[:, :, cols], res[:])
+            step = N // P // (2 if c == chunks - 1 else 1)
+            for i in range(0, N // P, step):
+                nc.scalar.activation(res[:, i : i + step], bank[:, i : i + step], ACT.Gelu_apprx_tanh)
+                nc.sync.dma_start(out_v[:, i : i + step, cols], res[:, i : i + step])
 
         th_second = stage.tile([P, per_half, CH, PACK], F32, name="raw")
         for c in range(chunks + 1):

@@ -25,6 +25,7 @@ SROWS = 4
 SHIFT = 16
 CH = 128
 HALF = 512
+FIRST_BANKS = 5
 
 
 def tile_list_unfollow_forecast_features_kernel(
@@ -38,12 +39,17 @@ def tile_list_unfollow_forecast_features_kernel(
 
     with ExitStack() as ctx:
         keep = ctx.enter_context(tc.tile_pool(name="keep", bufs=1))
-        stage = ctx.enter_context(tc.tile_pool(name="stage", bufs=2))
-        ps1 = ctx.enter_context(tc.psum_pool(name="ps1", bufs=5))
+        ps1 = ctx.enter_context(tc.psum_pool(name="ps1", bufs=1))
         ps2 = ctx.enter_context(tc.psum_pool(name="ps2", bufs=3))
 
         def sb(name, shape, dtype, tag=None):
             return keep.tile(shape, dtype, name=name, tag=tag or name, align_bytes=64)
+
+        turns = list(range(blocks * chunks + halves * PACK))
+
+        def first_stage_bank(shape):
+            name = "bank1_%d" % (turns.pop(0) % FIRST_BANKS)
+            return ps1.tile(shape, F32, name=name)
 
         list1 = keep.tile([P, S // 16], U16, name="list1")
         list2 = keep.tile([P, S // 16], U16, name="list2")
@@ -54,24 +60,6 @@ def tile_list_unfollow_forecast_features_kernel(
 
         def load_tab(a, c0, c1):
             nc.sync.dma_start(wwin[a][:, c0:c1].bitcast(I32), tab_words[a][:, 2 * c0 : 2 * c1].bitcast(I32))
-
-        nc.sync.dma_start(list1[:], offs)
-        for f in range(4):
-            load_tab(0, T // 4 * f, T // 4 * (f + 1))
-        nc.sync.dma_start(g1[:], gain1.rearrange("(b p t) -> p b t", b=blocks, t=PACK))
-        nc.sync.dma_start(b2[:], bias2.rearrange("(p t) -> p t", t=PACK))
-        nc.sync.dma_start(g2[:], gain2.rearrange("(p t) -> p t", t=PACK))
-
-        swin = sb("swin", [P, T], U8)
-        nc.vector.memset(swin[:].bitcast(I32), 0)
-        scale_rows = tab_scales.rearrange("a (q r) c -> r q a c", r=SROWS)
-        for r in range(SROWS):
-            nc.sync.dma_start(swin[r : P : SHIFT, :].bitcast(I32), scale_rows[r].bitcast(I32))
-
-        warm_in = sb("warm_in", [P, 1], F32)
-        warm_out = sb("warm_out", [P, 1], F32)
-        nc.gpsimd.memset(warm_in[:], 0.0)
-        nc.scalar.activation(warm_out[:], warm_in[:], ACT.Sigmoid)
 
         def zeroed(name, shape, tag=None):
             t = sb(name, shape, U8, tag)
@@ -85,15 +73,12 @@ def tile_list_unfollow_forecast_features_kernel(
                     scales[:, SROWS * q : SROWS * (q + 1), :].rearrange("a r c -> r a c").bitcast(I32),
                 )
 
-        s1 = [sb("s1_0", [P, S], U8), zeroed("s1_1", [P, S])]
-        s2 = [sb("s2_0", [P, S], U8), zeroed("s2_1", [P, S])]
-
         w1_raw = {}
         w1_codes = {}
         w1_scales = {}
 
         def load_w1(a, b):
-            raw = stage.tile([P, PACK, KP], F32, name="raw")
+            raw = sb("raw%d%d" % (a, b), [P, PACK, KP], F32, "raw00" if (a, b) == (1, 1) else None)
             nc.sync.dma_start(raw[:], w1[KP * a : KP * (a + 1), KP * b : KP * (b + 1)].rearrange("(p j) c -> p j c", j=PACK))
             w1_raw[a, b] = raw
 
@@ -103,18 +88,36 @@ def tile_list_unfollow_forecast_features_kernel(
                 grouped[:].rearrange("p (t m j) -> p m j t", t=PACK, j=PACK),
                 w1_raw[a, b][:].rearrange("p j (m t) -> p m j t", t=PACK),
             )
-            codes = sb("w1c%d%d" % (a, b), [P, KP], U32)
+            codes = sb("w1c%d%d" % (a, b), [P, KP], U32, "swin" if (a, b) == (1, 0) else None)
             scales = sb("w1s%d%d" % (a, b), [P, KP], U8)
             nc.vector.quantize_mx(out=codes[:].bitcast(FP8X4), scales=scales[:], in_=grouped[:])
             w1_codes[a, b] = codes
             w1_scales[a, b] = scales
 
-        load_w1(0, 0)
-        nc.sync.dma_start(list2[:], offs2)
-        load_w1(1, 0)
-        load_tab(1, 0, T)
+        swin = sb("swin", [P, T], U8)
+        nc.vector.memset(swin[:].bitcast(I32), 0)
+        warm_in = sb("warm_in", [P, 1], F32)
+        warm_out = sb("warm_out", [P, 1], F32)
+        nc.gpsimd.memset(warm_in[:], 0.0)
+        nc.scalar.activation(warm_out[:], warm_in[:], ACT.Sigmoid)
         w2s_raw = zeroed("w2s_raw", [P, passes, G])
+        s1 = [sb("s1_0", [P, S], U8), zeroed("s1_1", [P, S])]
+        s2 = [sb("s2_0", [P, S], U8), zeroed("s2_1", [P, S])]
+
+        nc.sync.dma_start(list1[:], offs)
+        load_tab(0, 0, T)
+        nc.sync.dma_start(list2[:], offs2)
+        scale_rows = tab_scales.rearrange("a (q r) c -> r q a c", r=SROWS)
+        for r in range(SROWS):
+            nc.sync.dma_start(swin[r : P : SHIFT, :].bitcast(I32), scale_rows[r].bitcast(I32))
+        load_w1(0, 0)
+        load_w1(1, 0)
         load_scale_rows(nc.sync, w2s_raw, w2_scales)
+        load_w1(0, 1)
+        load_tab(1, 0, T)
+        nc.sync.dma_start(g1[:], gain1.rearrange("(b p t) -> p b t", b=blocks, t=PACK))
+        nc.sync.dma_start(b2[:], bias2.rearrange("(p t) -> p t", t=PACK))
+        nc.sync.dma_start(g2[:], gain2.rearrange("(p t) -> p t", t=PACK))
 
         def gather_scales(planes, offsets):
             nc.vector.tensor_copy(planes[0][:], swin[:].indirect(offsets[:]))
@@ -124,37 +127,35 @@ def tile_list_unfollow_forecast_features_kernel(
         v2 = [sb("v2_%d" % a, [P, S], U16) for a in range(passes)]
         nc.vector.tensor_copy(v1[0][:], wwin[0][:].indirect(list1[:]))
         gather_scales(s1, list1)
-        prep_w1(0, 0)
         gather_scales(s2, list2)
-        load_w1(0, 1)
-        w2_raw = sb("w2_raw", [P, passes, G], I32, "w1bf00")
-        nc.sync.dma_start(w2_raw[:], w2_words.rearrange("a p c i -> p a (c i)").bitcast(I32))
-        prep_w1(1, 0)
         nc.vector.tensor_copy(v2[0][:], wwin[0][:].indirect(list2[:]))
+        prep_w1(0, 0)
         load_w1(1, 1)
-        w4_raw = sb("w4_raw", [P, PACK, N], F32, "w1bf10")
-        nc.sync.dma_start(w4_raw[:], w4.rearrange("(p j) n -> p j n", j=PACK))
+        prep_w1(1, 0)
+        w2_raw = sb("w2_raw", [P, passes, G], I32, "w1bf10")
+        nc.sync.dma_start(w2_raw[:], w2_words.rearrange("a p c i -> p a (c i)").bitcast(I32))
         for f in range(halves):
             nc.vector.tensor_copy(
                 v1[1][:, HALF * f : HALF * (f + 1)],
                 wwin[1][:].indirect(list1[:, HALF // 16 * f : HALF // 16 * (f + 1)]),
             )
-        nc.vector.tensor_copy(v2[1][:], wwin[1][:].indirect(list2[:]))
-
         prep_w1(0, 1)
+        w4_raw = sb("w4_raw", [P, PACK, N], F32, "w1bf01")
+        nc.sync.dma_start(w4_raw[:], w4.rearrange("(p j) n -> p j n", j=PACK))
+        nc.vector.tensor_copy(v2[1][:], wwin[1][:].indirect(list2[:]))
         prep_w1(1, 1)
-        w3s = zeroed("w3s", [P, blocks, N], "w1bf01")
+        w3s = zeroed("w3s", [P, blocks, N], "w1bf11")
         load_scale_rows(nc.sync, w3s, w3_scales)
-        w3c = sb("w3c", [P, blocks, 2 * N], U8, "w1bf11")
+        w3c = sb("w3c", [P, blocks, 2 * N], U8, "raw01")
         nc.sync.dma_start(w3c[:].bitcast(I32), w3_words.rearrange("a p n -> p a n").bitcast(I32))
 
-        h_bf = [sb("hbf%d" % b, [P, PACK * S], BF16) for b in range(blocks)]
+        h_bf = [sb("hbf0", [P, PACK * S], BF16, "w1bf10"), sb("hbf1", [P, PACK * S], BF16, "w1bf01")]
         h_codes = [sb("hc%d" % b, [P, S], U32) for b in range(blocks)]
         h_scales = [sb("hs%d" % b, [P, S], U8) for b in range(blocks)]
 
         def h_chunk(b, c, th):
             cols = slice(CH * c, CH * (c + 1))
-            bank = ps1.tile([P, PACK, CH], F32, name="bank1")
+            bank = first_stage_bank([P, PACK, CH])
             for t in range(PACK):
                 for a in range(passes):
                     nc.tensor.matmul_mx(
@@ -180,7 +181,7 @@ def tile_list_unfollow_forecast_features_kernel(
             )
 
         per_half = chunks // halves
-        th_first = stage.tile([P, per_half, CH, PACK], F32, name="raw")
+        th_first = sb("th_first", [P, per_half, CH, PACK], F32, "raw00")
         for c in range(per_half):
             h_chunk(0, c, th_first[:, c])
         quantize(h_codes[0], h_scales[0], h_bf[0], 0, HALF)
@@ -199,7 +200,7 @@ def tile_list_unfollow_forecast_features_kernel(
         for f in range(halves):
             sig = sb("sig%d" % f, [P, PACK, HALF], F32)
             for t in range(PACK):
-                bank = ps1.tile([P, HALF], F32, name="bank1")
+                bank = first_stage_bank([P, HALF])
                 for a in range(passes):
                     nc.tensor.matmul_mx(
                         out=bank[:],
@@ -261,7 +262,7 @@ def tile_list_unfollow_forecast_features_kernel(
                 nc.scalar.activation(res[:, i : i + step], bank[:, i : i + step], ACT.Gelu_apprx_tanh)
                 nc.sync.dma_start(out_v[:, i : i + step, cols], res[:, i : i + step])
 
-        th_second = stage.tile([P, per_half, CH, PACK], F32, name="raw")
+        th_second = sb("th_second", [P, per_half, CH, PACK], F32)
         for c in range(chunks + 1):
             if per_half <= c < chunks:
                 h_chunk(0, c, th_second[:, c - per_half])

@@ -25,6 +25,7 @@ SROWS = 4
 SHIFT = 16
 CH = 128
 HALF = 512
+BANKS = 8
 FIRST_BANKS = 5
 
 
@@ -39,17 +40,13 @@ def tile_list_unfollow_forecast_features_kernel(
 
     with ExitStack() as ctx:
         keep = ctx.enter_context(tc.tile_pool(name="keep", bufs=1))
-        ps1 = ctx.enter_context(tc.psum_pool(name="ps1", bufs=1))
-        ps2 = ctx.enter_context(tc.psum_pool(name="ps2", bufs=3))
+        psum = ctx.enter_context(tc.psum_pool(name="psum", bufs=1))
 
         def sb(name, shape, dtype, tag=None):
             return keep.tile(shape, dtype, name=name, tag=tag or name, align_bytes=64)
 
-        turns = list(range(blocks * chunks + halves * PACK))
-
-        def first_stage_bank(shape):
-            name = "bank1_%d" % (turns.pop(0) % FIRST_BANKS)
-            return ps1.tile(shape, F32, name=name)
+        def bank_tile(index, shape):
+            return psum.tile(shape, F32, name="bank%d" % index)
 
         list1 = keep.tile([P, S // 16], U16, name="list1")
         list2 = keep.tile([P, S // 16], U16, name="list2")
@@ -74,25 +71,29 @@ def tile_list_unfollow_forecast_features_kernel(
                 )
 
         w1_raw = {}
-        w1_codes = {}
-        w1_scales = {}
 
         def load_w1(a, b):
-            raw = sb("raw%d%d" % (a, b), [P, PACK, KP], F32, "raw00" if (a, b) == (1, 1) else None)
+            raw = sb("raw%d%d" % (a, b), [P, PACK, KP], F32)
             nc.sync.dma_start(raw[:], w1[KP * a : KP * (a + 1), KP * b : KP * (b + 1)].rearrange("(p j) c -> p j c", j=PACK))
             w1_raw[a, b] = raw
 
-        def prep_w1(a, b):
-            grouped = sb("w1bf%d%d" % (a, b), [P, PACK * KP], BF16)
+        def cast_w1(a, b, grouped):
             nc.scalar.copy(
-                grouped[:].rearrange("p (t m j) -> p m j t", t=PACK, j=PACK),
+                grouped.rearrange("p (t m j) -> p m j t", t=PACK, j=PACK),
                 w1_raw[a, b][:].rearrange("p j (m t) -> p m j t", t=PACK),
             )
-            codes = sb("w1c%d%d" % (a, b), [P, KP], U32, "swin" if (a, b) == (1, 0) else None)
-            scales = sb("w1s%d%d" % (a, b), [P, KP], U8)
-            nc.vector.quantize_mx(out=codes[:].bitcast(FP8X4), scales=scales[:], in_=grouped[:])
-            w1_codes[a, b] = codes
-            w1_scales[a, b] = scales
+
+        def quantize(codes, scales, values, c0, c1):
+            nc.vector.quantize_mx(
+                out=codes[:, c0:c1].bitcast(FP8X4), scales=scales[:, c0:c1], in_=values[:, PACK * c0 : PACK * c1]
+            )
+
+        w1_bf = [sb("w1bf%d" % b, [P, passes * PACK * KP], BF16) for b in range(blocks)]
+        w1_codes = [sb("w1c%d" % b, [P, passes * KP], U32) for b in range(blocks)]
+        w1_scales = [sb("w1s%d" % b, [P, passes * KP], U8) for b in range(blocks)]
+
+        def cast_piece(a, b):
+            cast_w1(a, b, w1_bf[b][:, PACK * KP * a : PACK * KP * (a + 1)])
 
         swin = sb("swin", [P, T], U8)
         nc.vector.memset(swin[:].bitcast(I32), 0)
@@ -104,69 +105,84 @@ def tile_list_unfollow_forecast_features_kernel(
         s1 = [sb("s1_0", [P, S], U8), zeroed("s1_1", [P, S])]
         s2 = [sb("s2_0", [P, S], U8), zeroed("s2_1", [P, S])]
 
+        def gather_scales(planes, offsets):
+            nc.vector.tensor_copy(planes[0][:], swin[:].indirect(offsets[:]))
+
+        def move_scales(planes):
+            nc.sync.dma_start(planes[1][0 : P - SHIFT, :].bitcast(I32), planes[0][SHIFT:P, :].bitcast(I32))
+
+        v1 = [sb("v1_%d" % a, [P, S], U16) for a in range(passes)]
+        w2_raw = sb("w2_raw", [P, passes, G], I32)
+        v2 = [sb("v2_0", [P, S], U16), sb("v2_1", [P, S], U16, "w2_raw")]
+        w4_raw = sb("w4_raw", [P, PACK, N], F32)
+        w3s = zeroed("w3s", [P, blocks, N])
+        w3c = sb("w3c", [P, blocks, 2 * N], U8)
+        w2c = sb("w2c", [P, passes, G], I32)
+        w2s = sb("w2s", [P, passes, G], U8)
+
         nc.sync.dma_start(list1[:], offs)
         load_tab(0, 0, T)
-        nc.sync.dma_start(list2[:], offs2)
         scale_rows = tab_scales.rearrange("a (q r) c -> r q a c", r=SROWS)
         for r in range(SROWS):
             nc.sync.dma_start(swin[r : P : SHIFT, :].bitcast(I32), scale_rows[r].bitcast(I32))
         load_w1(0, 0)
+        nc.sync.dma_start(list2[:], offs2)
         load_w1(1, 0)
-        load_scale_rows(nc.sync, w2s_raw, w2_scales)
         load_w1(0, 1)
         load_tab(1, 0, T)
-        nc.sync.dma_start(g1[:], gain1.rearrange("(b p t) -> p b t", b=blocks, t=PACK))
-        nc.sync.dma_start(b2[:], bias2.rearrange("(p t) -> p t", t=PACK))
-        nc.sync.dma_start(g2[:], gain2.rearrange("(p t) -> p t", t=PACK))
+        load_scale_rows(nc.sync, w2s_raw, w2_scales)
 
-        def gather_scales(planes, offsets):
-            nc.vector.tensor_copy(planes[0][:], swin[:].indirect(offsets[:]))
-            nc.sync.dma_start(planes[1][0 : P - SHIFT, :].bitcast(I32), planes[0][SHIFT:P, :].bitcast(I32))
-
-        v1 = [sb("v1_%d" % a, [P, S], U16) for a in range(passes)]
-        v2 = [sb("v2_%d" % a, [P, S], U16) for a in range(passes)]
         nc.vector.tensor_copy(v1[0][:], wwin[0][:].indirect(list1[:]))
         gather_scales(s1, list1)
         gather_scales(s2, list2)
         nc.vector.tensor_copy(v2[0][:], wwin[0][:].indirect(list2[:]))
-        prep_w1(0, 0)
-        load_w1(1, 1)
-        prep_w1(1, 0)
-        w2_raw = sb("w2_raw", [P, passes, G], I32, "w1bf10")
+        move_scales(s1)
+        move_scales(s2)
         nc.sync.dma_start(w2_raw[:], w2_words.rearrange("a p c i -> p a (c i)").bitcast(I32))
+        load_w1(1, 1)
+        nc.sync.dma_start(g1[:], gain1.rearrange("(b p t) -> p b t", b=blocks, t=PACK))
+        nc.sync.dma_start(b2[:], bias2.rearrange("(p t) -> p t", t=PACK))
+        nc.sync.dma_start(g2[:], gain2.rearrange("(p t) -> p t", t=PACK))
+        nc.sync.dma_start(w4_raw[:], w4.rearrange("(p j) n -> p j n", j=PACK))
+        load_scale_rows(nc.sync, w3s, w3_scales)
+        nc.sync.dma_start(w3c[:].bitcast(I32), w3_words.rearrange("a p n -> p a n").bitcast(I32))
+
+        for a in range(passes):
+            cast_piece(a, 0)
+            quantize(w1_codes[0], w1_scales[0], w1_bf[0], KP * a, KP * (a + 1))
+        cast_piece(0, 1)
         for f in range(halves):
             nc.vector.tensor_copy(
                 v1[1][:, HALF * f : HALF * (f + 1)],
                 wwin[1][:].indirect(list1[:, HALF // 16 * f : HALF // 16 * (f + 1)]),
             )
-        prep_w1(0, 1)
-        w4_raw = sb("w4_raw", [P, PACK, N], F32, "w1bf01")
-        nc.sync.dma_start(w4_raw[:], w4.rearrange("(p j) n -> p j n", j=PACK))
+        nc.vector.tensor_copy(
+            w2s[:].rearrange("p a (t m) -> p a m t", t=PACK), w2s_raw[:].rearrange("p a (m t) -> p a m t", t=PACK)
+        )
+        nc.vector.tensor_copy(
+            w2c[:].rearrange("p a (t m) -> p a m t", t=PACK), w2_raw[:].rearrange("p a (m t) -> p a m t", t=PACK)
+        )
         nc.vector.tensor_copy(v2[1][:], wwin[1][:].indirect(list2[:]))
-        prep_w1(1, 1)
-        w3s = zeroed("w3s", [P, blocks, N], "w1bf11")
-        load_scale_rows(nc.sync, w3s, w3_scales)
-        w3c = sb("w3c", [P, blocks, 2 * N], U8, "raw01")
-        nc.sync.dma_start(w3c[:].bitcast(I32), w3_words.rearrange("a p n -> p a n").bitcast(I32))
 
-        h_bf = [sb("hbf0", [P, PACK * S], BF16, "w1bf10"), sb("hbf1", [P, PACK * S], BF16, "w1bf01")]
+        h_bf = [sb("hbf0", [P, PACK * S], BF16), sb("hbf1", [P, PACK * S], BF16, "w4_raw")]
         h_codes = [sb("hc%d" % b, [P, S], U32) for b in range(blocks)]
         h_scales = [sb("hs%d" % b, [P, S], U8) for b in range(blocks)]
 
-        def h_chunk(b, c, th):
+        def h_pass(bank, b, c, a):
             cols = slice(CH * c, CH * (c + 1))
-            bank = first_stage_bank([P, PACK, CH])
             for t in range(PACK):
-                for a in range(passes):
-                    nc.tensor.matmul_mx(
-                        out=bank[:, t, :],
-                        lhsT=w1_codes[a, b][:, P * t : P * (t + 1)].bitcast(FP8X4),
-                        lhsT_scale=w1_scales[a, b][:, P * t : P * (t + 1)],
-                        rhs=v1[a][:, cols].bitcast(FP4X4),
-                        rhs_scale=s1[a][:, cols],
-                        start=(a == 0),
-                        stop=(a == passes - 1),
-                    )
+                rows = slice(KP * a + P * t, KP * a + P * (t + 1))
+                nc.tensor.matmul_mx(
+                    out=bank[:, t, :],
+                    lhsT=w1_codes[b][:, rows].bitcast(FP8X4),
+                    lhsT_scale=w1_scales[b][:, rows],
+                    rhs=v1[a][:, cols].bitcast(FP4X4),
+                    rhs_scale=s1[a][:, cols],
+                    start=(a == 0 and t == 0),
+                    stop=(a == passes - 1 and t == PACK - 1),
+                )
+
+        def h_finish(bank, b, c, th):
             nc.scalar.activation(th, bank[:].rearrange("p t n -> p n t"), ACT.Tanh)
             nc.vector.tensor_tensor(
                 h_bf[b][:, PACK * CH * c : PACK * CH * (c + 1)].rearrange("p (n t) -> p n t", t=PACK),
@@ -175,43 +191,42 @@ def tile_list_unfollow_forecast_features_kernel(
                 MULT,
             )
 
-        def quantize(codes, scales, values, c0, c1):
-            nc.vector.quantize_mx(
-                out=codes[:, c0:c1].bitcast(FP8X4), scales=scales[:, c0:c1], in_=values[:, PACK * c0 : PACK * c1]
-            )
-
         per_half = chunks // halves
-        th_first = sb("th_first", [P, per_half, CH, PACK], F32, "raw00")
+        th_first = sb("th_first", [P, per_half, CH, PACK], F32)
+        first = [bank_tile(c, [P, PACK, CH]) for c in range(per_half)]
         for c in range(per_half):
-            h_chunk(0, c, th_first[:, c])
+            h_pass(first[c], 0, c, 0)
+        for c in range(per_half):
+            h_pass(first[c], 0, c, 1)
+            h_finish(first[c], 0, c, th_first[:, c])
+        cast_piece(1, 1)
         quantize(h_codes[0], h_scales[0], h_bf[0], 0, HALF)
+        quantize(w1_codes[1], w1_scales[1], w1_bf[1], 0, passes * KP)
 
-        w2c = sb("w2c", [P, passes, G], I32)
-        w2s = sb("w2s", [P, passes, G], U8)
-        nc.vector.tensor_copy(
-            w2c[:].rearrange("p a (t m) -> p a m t", t=PACK), w2_raw[:].rearrange("p a (m t) -> p a m t", t=PACK)
-        )
-        nc.vector.tensor_copy(
-            w2s[:].rearrange("p a (t m) -> p a m t", t=PACK), w2s_raw[:].rearrange("p a (m t) -> p a m t", t=PACK)
-        )
         d_bf = sb("dbf", [P, PACK * S], BF16)
         d_codes = sb("dc", [P, S], U32)
         d_scales = sb("ds", [P, S], U8)
+        d_banks = [[bank_tile((PACK * (f + 1) + t) % BANKS, [P, HALF]) for t in range(PACK)] for f in range(halves)]
+
+        def d_pass(f, t, a):
+            nc.tensor.matmul_mx(
+                out=d_banks[f][t][:],
+                lhsT=w2c[:, a, P * t : P * (t + 1)].bitcast(FP8X4),
+                lhsT_scale=w2s[:, a, P * t : P * (t + 1)],
+                rhs=v2[a][:, HALF * f : HALF * (f + 1)].bitcast(FP4X4),
+                rhs_scale=s2[a][:, HALF * f : HALF * (f + 1)],
+                start=(a == 0),
+                stop=(a == passes - 1),
+            )
+
         for f in range(halves):
-            sig = sb("sig%d" % f, [P, PACK, HALF], F32)
             for t in range(PACK):
-                bank = first_stage_bank([P, HALF])
-                for a in range(passes):
-                    nc.tensor.matmul_mx(
-                        out=bank[:],
-                        lhsT=w2c[:, a, P * t : P * (t + 1)].bitcast(FP8X4),
-                        lhsT_scale=w2s[:, a, P * t : P * (t + 1)],
-                        rhs=v2[a][:, HALF * f : HALF * (f + 1)].bitcast(FP4X4),
-                        rhs_scale=s2[a][:, HALF * f : HALF * (f + 1)],
-                        start=(a == 0),
-                        stop=(a == passes - 1),
-                    )
-                nc.scalar.activation(sig[:, t, :], bank[:], ACT.Sigmoid, bias=b2[:, t : t + 1])
+                d_pass(f, t, 0)
+        for f in range(halves):
+            sig = sb("sig%d" % f, [P, PACK, HALF], F32, "raw11" if f == 0 else None)
+            for t in range(PACK):
+                d_pass(f, t, 1)
+                nc.scalar.activation(sig[:, t, :], d_banks[f][t][:], ACT.Sigmoid, bias=b2[:, t : t + 1])
             nc.vector.tensor_tensor(
                 d_bf[:, PACK * HALF * f : PACK * HALF * (f + 1)].rearrange("p (c i t) -> p c t i", i=PACK, t=PACK),
                 sig[:].rearrange("p t (c i) -> p c t i", i=PACK),
@@ -233,7 +248,7 @@ def tile_list_unfollow_forecast_features_kernel(
 
         def y_chunk(c):
             cols = slice(CH * c, CH * (c + 1))
-            bank = ps2.tile([P, N // P, CH], F32, name="bank2")
+            bank = bank_tile(FIRST_BANKS + c % (BANKS - FIRST_BANKS), [P, N // P, CH])
             for i in range(N // P):
                 rows = slice(P * i, P * (i + 1))
                 nc.tensor.matmul_mx(
@@ -261,6 +276,14 @@ def tile_list_unfollow_forecast_features_kernel(
             for i in range(0, N // P, step):
                 nc.scalar.activation(res[:, i : i + step], bank[:, i : i + step], ACT.Gelu_apprx_tanh)
                 nc.sync.dma_start(out_v[:, i : i + step, cols], res[:, i : i + step])
+
+        turns = list(range(FIRST_BANKS - 1, FIRST_BANKS - 1 + chunks + per_half))
+
+        def h_chunk(b, c, th):
+            bank = bank_tile(turns.pop(0) % FIRST_BANKS, [P, PACK, CH])
+            for a in range(passes):
+                h_pass(bank, b, c, a)
+            h_finish(bank, b, c, th)
 
         th_second = sb("th_second", [P, per_half, CH, PACK], F32)
         for c in range(chunks + 1):

@@ -122,23 +122,23 @@ def tile_list_unfollow_forecast_features_kernel(
 
         nc.sync.dma_start(list1[:], offs)
         load_tab(0, 0, T)
+        nc.sync.dma_start(list2[:], offs2)
         scale_rows = tab_scales.rearrange("a (q r) c -> r q a c", r=SROWS)
         for r in range(SROWS):
             nc.sync.dma_start(swin[r : P : SHIFT, :].bitcast(I32), scale_rows[r].bitcast(I32))
         load_w1(0, 0)
-        nc.sync.dma_start(list2[:], offs2)
         load_w1(1, 0)
-        load_w1(0, 1)
         load_tab(1, 0, T)
+        load_w1(0, 1)
         load_scale_rows(nc.sync, w2s_raw, w2_scales)
 
         nc.vector.tensor_copy(v1[0][:], wwin[0][:].indirect(list1[:]))
+        nc.vector.tensor_copy(v2[0][:], wwin[0][:].indirect(list2[:]))
         gather_scales(s1, list1)
         gather_scales(s2, list2)
-        nc.vector.tensor_copy(v2[0][:], wwin[0][:].indirect(list2[:]))
         move_scales(s1)
-        move_scales(s2)
         nc.sync.dma_start(w2_raw[:], w2_words.rearrange("a p c i -> p a (c i)").bitcast(I32))
+        move_scales(s2)
         load_w1(1, 1)
         nc.sync.dma_start(g1[:], gain1.rearrange("(b p t) -> p b t", b=blocks, t=PACK))
         nc.sync.dma_start(b2[:], bias2.rearrange("(p t) -> p t", t=PACK))

@@ -22,11 +22,10 @@ KP = P * PACK
 QUADS = 4
 QUAD = 32
 SROWS = 4
-SHIFT = 16
-CH = 128
+LIVE = 96
+CH = 256
 HALF = 512
-BANKS = 8
-FIRST_BANKS = 5
+BANK = 512
 
 
 def tile_list_unfollow_forecast_features_kernel(
@@ -35,7 +34,6 @@ def tile_list_unfollow_forecast_features_kernel(
     nc = tc.nc
     passes = K // KP
     blocks = H // KP
-    chunks = S // CH
     halves = S // HALF
 
     with ExitStack() as ctx:
@@ -45,30 +43,46 @@ def tile_list_unfollow_forecast_features_kernel(
         def sb(name, shape, dtype, tag=None):
             return keep.tile(shape, dtype, name=name, tag=tag or name, align_bytes=64)
 
-        def bank_tile(index, shape):
+        def bank(index, shape):
             return psum.tile(shape, F32, name="bank%d" % index)
 
         list1 = keep.tile([P, S // 16], U16, name="list1")
         list2 = keep.tile([P, S // 16], U16, name="list2")
         wwin = [sb("wwin%d" % a, [P, T], U16) for a in range(passes)]
+        swin = sb("swin", [P, T], U8)
+        picked = sb("picked", [P, 2, S], U8)
+        planes = [sb("plane%d" % a, [P, 2, S], U8) for a in range(passes)]
         g1 = sb("g1", [P, blocks, PACK], F32)
         g2 = sb("g2", [P, PACK], F32)
         b2 = sb("b2", [P, PACK], F32)
+        w2s_raw = sb("w2s_raw", [P, passes, G], U8)
+        w3s = sb("w3s", [P, blocks, N], U8)
+        w2_raw = sb("w2_raw", [P, passes, G], I32)
+        w2c = sb("w2c", [P, passes, G], U32)
+        w2s = sb("w2s", [P, passes, G], U8)
+        w4_raw = sb("w4_raw", [P, PACK, N], F32)
+        w3c = sb("w3c", [P, blocks, 2 * N], U8)
 
-        def load_tab(a, c0, c1):
-            nc.sync.dma_start(wwin[a][:, c0:c1].bitcast(I32), tab_words[a][:, 2 * c0 : 2 * c1].bitcast(I32))
+        nc.vector.memset(swin[0:LIVE].bitcast(I32), 0)
+        for a in range(passes):
+            nc.vector.memset(planes[a][:].bitcast(I32), 0)
+        warm_in = sb("warm_in", [P, 1], F32)
+        warm_out = sb("warm_out", [P, 1], F32)
+        nc.gpsimd.memset(warm_in[:], 0.0)
+        nc.scalar.activation(warm_out[:], warm_in[:], ACT.Sigmoid)
 
-        def zeroed(name, shape, tag=None):
-            t = sb(name, shape, U8, tag)
-            nc.gpsimd.memset(t[:].bitcast(I32), 0)
-            return t
-
-        def load_scale_rows(queue, plane, scales):
+        def load_scale_rows(plane, scales):
             for q in range(QUADS):
-                queue.dma_start(
+                nc.sync.dma_start(
                     plane[QUAD * q : QUAD * q + SROWS].bitcast(I32),
                     scales[:, SROWS * q : SROWS * (q + 1), :].rearrange("a r c -> r a c").bitcast(I32),
                 )
+
+        nc.gpsimd.memset(w2s_raw[:].bitcast(I32), 0)
+        nc.gpsimd.memset(w3s[:].bitcast(I32), 0)
+
+        def load_tab(a):
+            nc.sync.dma_start(wwin[a][:].bitcast(I32), tab_words[a].bitcast(I32))
 
         w1_raw = {}
 
@@ -77,223 +91,282 @@ def tile_list_unfollow_forecast_features_kernel(
             nc.sync.dma_start(raw[:], w1[KP * a : KP * (a + 1), KP * b : KP * (b + 1)].rearrange("(p j) c -> p j c", j=PACK))
             w1_raw[a, b] = raw
 
-        def cast_w1(a, b, grouped):
+        def move_scales(a):
+            for q in range(QUADS):
+                row = LIVE + QUADS * SROWS * a + SROWS * q
+                nc.sync.dma_start(
+                    planes[a][QUAD * q : QUAD * q + SROWS].bitcast(I32), picked[row : row + SROWS].bitcast(I32)
+                )
+
+        def quantize(name, values, tag=None):
+            width = values.shape[1] // PACK
+            codes = sb(name + "c", [P, width], U32, tag)
+            scales = sb(name + "s", [P, width], U8)
+            nc.vector.quantize_mx(out=codes[:].bitcast(FP8X4), scales=scales[:], in_=values)
+            return codes, scales
+
+        w1_bf = {}
+        w1_q = {}
+
+        def cast_w1(a, b, tag=None):
+            grouped = sb("w1bf%d%d" % (a, b), [P, PACK * KP], BF16, tag)
             nc.scalar.copy(
-                grouped.rearrange("p (t m j) -> p m j t", t=PACK, j=PACK),
+                grouped[:].rearrange("p (t m j) -> p m j t", t=PACK, j=PACK),
                 w1_raw[a, b][:].rearrange("p j (m t) -> p m j t", t=PACK),
             )
+            w1_bf[a, b] = grouped
 
-        def quantize(codes, scales, values, c0, c1):
-            nc.vector.quantize_mx(
-                out=codes[:, c0:c1].bitcast(FP8X4), scales=scales[:, c0:c1], in_=values[:, PACK * c0 : PACK * c1]
-            )
+        def quantize_w1(a, b):
+            w1_q[a, b] = quantize("w1q%d%d" % (a, b), w1_bf[a, b][:])
 
-        w1_bf = [sb("w1bf%d" % b, [P, passes * PACK * KP], BF16) for b in range(blocks)]
-        w1_codes = [sb("w1c%d" % b, [P, passes * KP], U32) for b in range(blocks)]
-        w1_scales = [sb("w1s%d" % b, [P, passes * KP], U8) for b in range(blocks)]
-
-        def cast_piece(a, b):
-            cast_w1(a, b, w1_bf[b][:, PACK * KP * a : PACK * KP * (a + 1)])
-
-        swin = sb("swin", [P, T], U8)
-        nc.vector.memset(swin[:].bitcast(I32), 0)
-        warm_in = sb("warm_in", [P, 1], F32)
-        warm_out = sb("warm_out", [P, 1], F32)
-        nc.gpsimd.memset(warm_in[:], 0.0)
-        nc.scalar.activation(warm_out[:], warm_in[:], ACT.Sigmoid)
-        w2s_raw = zeroed("w2s_raw", [P, passes, G])
-        s1 = [sb("s1_0", [P, S], U8), zeroed("s1_1", [P, S])]
-        s2 = [sb("s2_0", [P, S], U8), zeroed("s2_1", [P, S])]
-
-        def gather_scales(planes, offsets):
-            nc.vector.tensor_copy(planes[0][:], swin[:].indirect(offsets[:]))
-
-        def move_scales(planes):
-            nc.sync.dma_start(planes[1][0 : P - SHIFT, :].bitcast(I32), planes[0][SHIFT:P, :].bitcast(I32))
-
-        v1 = [sb("v1_%d" % a, [P, S], U16) for a in range(passes)]
-        w2_raw = sb("w2_raw", [P, passes, G], I32)
-        v2 = [sb("v2_0", [P, S], U16), sb("v2_1", [P, S], U16, "w2_raw")]
-        w4_raw = sb("w4_raw", [P, PACK, N], F32)
-        w3s = zeroed("w3s", [P, blocks, N])
-        w3c = sb("w3c", [P, blocks, 2 * N], U8)
-        w2c = sb("w2c", [P, passes, G], I32)
-        w2s = sb("w2s", [P, passes, G], U8)
+        def gather(dst, window, offsets, c0, c1):
+            nc.vector.tensor_copy(dst, window[:].indirect(offsets[:, c0 // 16 : c1 // 16]))
 
         nc.sync.dma_start(list1[:], offs)
-        load_tab(0, 0, T)
+        nc.sync.dma_start(swin[LIVE:P].bitcast(I32), tab_scales.rearrange("a r c -> (a r) c").bitcast(I32))
         nc.sync.dma_start(list2[:], offs2)
-        scale_rows = tab_scales.rearrange("a (q r) c -> r q a c", r=SROWS)
-        for r in range(SROWS):
-            nc.sync.dma_start(swin[r : P : SHIFT, :].bitcast(I32), scale_rows[r].bitcast(I32))
+        load_tab(0)
+        load_scale_rows(w2s_raw, w2_scales)
+        nc.sync.dma_start(g1[:], gain1.rearrange("(b p t) -> p b t", b=blocks, t=PACK))
         load_w1(0, 0)
         load_w1(1, 0)
-        load_tab(1, 0, T)
-        load_w1(0, 1)
-        load_scale_rows(nc.sync, w2s_raw, w2_scales)
 
-        nc.vector.tensor_copy(v1[0][:], wwin[0][:].indirect(list1[:]))
-        nc.vector.tensor_copy(v2[0][:], wwin[0][:].indirect(list2[:]))
-        gather_scales(s1, list1)
-        gather_scales(s2, list2)
-        move_scales(s1)
+        gather(picked[:, 0, :], swin, list1, 0, S)
+        gather(picked[:, 1, :], swin, list2, 0, S)
+        move_scales(0)
+        load_tab(1)
+        load_w1(0, 1)
+        move_scales(1)
         nc.sync.dma_start(w2_raw[:], w2_words.rearrange("a p c i -> p a (c i)").bitcast(I32))
-        move_scales(s2)
         load_w1(1, 1)
-        nc.sync.dma_start(g1[:], gain1.rearrange("(b p t) -> p b t", b=blocks, t=PACK))
         nc.sync.dma_start(b2[:], bias2.rearrange("(p t) -> p t", t=PACK))
         nc.sync.dma_start(g2[:], gain2.rearrange("(p t) -> p t", t=PACK))
         nc.sync.dma_start(w4_raw[:], w4.rearrange("(p j) n -> p j n", j=PACK))
-        load_scale_rows(nc.sync, w3s, w3_scales)
         nc.sync.dma_start(w3c[:].bitcast(I32), w3_words.rearrange("a p n -> p a n").bitcast(I32))
+        load_scale_rows(w3s, w3_scales)
 
-        for a in range(passes):
-            cast_piece(a, 0)
-            quantize(w1_codes[0], w1_scales[0], w1_bf[0], KP * a, KP * (a + 1))
-        cast_piece(0, 1)
-        for f in range(halves):
-            nc.vector.tensor_copy(
-                v1[1][:, HALF * f : HALF * (f + 1)],
-                wwin[1][:].indirect(list1[:, HALF // 16 * f : HALF // 16 * (f + 1)]),
-            )
+        v1 = [sb("v1_%d" % a, [P, S], U16) for a in range(passes)]
+        v2 = {}
+
+        def gather_v2(a, tag=None):
+            v2[a] = sb("v2_%d" % a, [P, S], U16, tag)
+            gather(v2[a][:], wwin[a], list2, 0, S)
+
+        gather(v1[0][:], wwin[0], list1, 0, S)
         nc.vector.tensor_copy(
             w2s[:].rearrange("p a (t m) -> p a m t", t=PACK), w2s_raw[:].rearrange("p a (m t) -> p a m t", t=PACK)
         )
-        nc.vector.tensor_copy(
-            w2c[:].rearrange("p a (t m) -> p a m t", t=PACK), w2_raw[:].rearrange("p a (m t) -> p a m t", t=PACK)
+        cast_w1(0, 0)
+        quantize_w1(0, 0)
+        gather_v2(0, "w1bf00")
+        cast_w1(1, 0)
+        quantize_w1(1, 0)
+        cast_w1(0, 1)
+        nc.scalar.copy(
+            w2c[:].rearrange("p a (t m) -> p a m t", t=PACK),
+            w2_raw[:].bitcast(U32).rearrange("p a (m t) -> p a m t", t=PACK),
         )
-        nc.vector.tensor_copy(v2[1][:], wwin[1][:].indirect(list2[:]))
+        for f in range(halves):
+            gather(v1[1][:, HALF * f : HALF * (f + 1)], wwin[1], list1, HALF * f, HALF * (f + 1))
+        gather_v2(1)
 
-        h_bf = [sb("hbf0", [P, PACK * S], BF16), sb("hbf1", [P, PACK * S], BF16, "w4_raw")]
-        h_codes = [sb("hc%d" % b, [P, S], U32) for b in range(blocks)]
-        h_scales = [sb("hs%d" % b, [P, S], U8) for b in range(blocks)]
+        early_bf = sb("early_bf", [P, PACK * HALF], BF16)
+        late_bf = sb("late_bf", [P, PACK * S], BF16)
+        h1_bf = sb("h1_bf", [P, PACK * S], BF16)
 
-        def h_pass(bank, b, c, a):
-            cols = slice(CH * c, CH * (c + 1))
+        def h_bf(b, c0, width):
+            tile = h1_bf if b == 1 else early_bf if c0 < HALF else late_bf
+            return tile[:, PACK * c0 : PACK * (c0 + width)]
+
+        def h_banks(first, width):
+            per = BANK // width
+            return [bank(first + u, [P, per, width]) for u in range(PACK // per)]
+
+        def h_pass(banks, b, c0, width, a):
+            per = BANK // width
+            codes, scales = w1_q[a, b]
             for t in range(PACK):
-                rows = slice(KP * a + P * t, KP * a + P * (t + 1))
                 nc.tensor.matmul_mx(
-                    out=bank[:, t, :],
-                    lhsT=w1_codes[b][:, rows].bitcast(FP8X4),
-                    lhsT_scale=w1_scales[b][:, rows],
-                    rhs=v1[a][:, cols].bitcast(FP4X4),
-                    rhs_scale=s1[a][:, cols],
-                    start=(a == 0 and t == 0),
-                    stop=(a == passes - 1 and t == PACK - 1),
+                    out=banks[t // per][:, t % per, :],
+                    lhsT=codes[:, P * t : P * (t + 1)].bitcast(FP8X4),
+                    lhsT_scale=scales[:, P * t : P * (t + 1)],
+                    rhs=v1[a][:, c0 : c0 + width].bitcast(FP4X4),
+                    rhs_scale=planes[a][:, 0, c0 : c0 + width],
+                    start=(a == 0 and t % per == 0),
+                    stop=(a == passes - 1 and t % per == per - 1),
                 )
 
-        def h_finish(bank, b, c, th):
-            nc.scalar.activation(th, bank[:].rearrange("p t n -> p n t"), ACT.Tanh)
+        th = {}
+
+        def h_tanh(banks, b, c0):
+            for u in range(len(banks)):
+                nc.scalar.activation(th[b, c0][:, u], banks[u][:].rearrange("p e n -> p n e"), ACT.Tanh)
+
+        def h_first(first, b, c0, width):
+            banks = h_banks(first, width)
+            for a in range(passes):
+                h_pass(banks, b, c0, width, a)
+            th[b, c0] = sb("th%d_%d" % (b, c0), [P, len(banks), width, PACK // len(banks)], F32)[:]
+            h_tanh(banks, b, c0)
+
+        def h_gain(b, c0, width):
+            per = BANK // width
             nc.vector.tensor_tensor(
-                h_bf[b][:, PACK * CH * c : PACK * CH * (c + 1)].rearrange("p (n t) -> p n t", t=PACK),
-                th,
-                g1[:, b : b + 1, :].to_broadcast([P, CH, PACK]),
+                h_bf(b, c0, width).rearrange("p (n u e) -> p n u e", u=PACK // per, e=per),
+                th[b, c0].rearrange("p u n e -> p n u e"),
+                g1[:, b : b + 1, :].rearrange("p n (u e) -> p n u e", e=per).to_broadcast([P, width, PACK // per, per]),
                 MULT,
             )
 
-        per_half = chunks // halves
-        th_first = sb("th_first", [P, per_half, CH, PACK], F32)
-        first = [bank_tile(c, [P, PACK, CH]) for c in range(per_half)]
-        for c in range(per_half):
-            h_pass(first[c], 0, c, 0)
-        for c in range(per_half):
-            h_pass(first[c], 0, c, 1)
-            h_finish(first[c], 0, c, th_first[:, c])
-        cast_piece(1, 1)
-        quantize(h_codes[0], h_scales[0], h_bf[0], 0, HALF)
-        quantize(w1_codes[1], w1_scales[1], w1_bf[1], 0, passes * KP)
+        h_q = {}
 
-        d_bf = sb("dbf", [P, PACK * S], BF16)
-        d_codes = sb("dc", [P, S], U32)
-        d_scales = sb("ds", [P, S], U8)
-        d_banks = [[bank_tile((PACK * (f + 1) + t) % BANKS, [P, HALF]) for t in range(PACK)] for f in range(halves)]
+        def h_quantize(b, c0, width, tag):
+            codes, scales = quantize("hq%d_%d" % (b, c0), h_bf(b, c0, width), tag)
+            for c in range(c0, c0 + width, P):
+                h_q[b, c] = (codes, scales, c - c0)
 
-        def d_pass(f, t, a):
+        def d_pass(banks, f, t, a):
             nc.tensor.matmul_mx(
-                out=d_banks[f][t][:],
+                out=banks[t][:],
                 lhsT=w2c[:, a, P * t : P * (t + 1)].bitcast(FP8X4),
                 lhsT_scale=w2s[:, a, P * t : P * (t + 1)],
                 rhs=v2[a][:, HALF * f : HALF * (f + 1)].bitcast(FP4X4),
-                rhs_scale=s2[a][:, HALF * f : HALF * (f + 1)],
+                rhs_scale=planes[a][:, 1, HALF * f : HALF * (f + 1)],
                 start=(a == 0),
                 stop=(a == passes - 1),
             )
 
-        for f in range(halves):
+        def d_sigmoid(banks, sig):
             for t in range(PACK):
-                d_pass(f, t, 0)
-        for f in range(halves):
-            sig = sb("sig%d" % f, [P, PACK, HALF], F32, "raw11" if f == 0 else None)
-            for t in range(PACK):
-                d_pass(f, t, 1)
-                nc.scalar.activation(sig[:, t, :], d_banks[f][t][:], ACT.Sigmoid, bias=b2[:, t : t + 1])
+                nc.scalar.activation(sig[:, t, :], banks[t][:], ACT.Sigmoid, bias=b2[:, t : t + 1])
+
+        def d_gain(dst, sig):
             nc.vector.tensor_tensor(
-                d_bf[:, PACK * HALF * f : PACK * HALF * (f + 1)].rearrange("p (c i t) -> p c t i", i=PACK, t=PACK),
-                sig[:].rearrange("p t (c i) -> p c t i", i=PACK),
+                dst.rearrange("p (c i t) -> p c t i", i=PACK, t=PACK),
+                sig.rearrange("p t (c i) -> p c t i", i=PACK),
                 g2[:].rearrange("p (c t i) -> p c t i", c=1, i=1).to_broadcast([P, HALF // PACK, PACK, PACK]),
                 MULT,
             )
-            quantize(d_codes, d_scales, d_bf, HALF * f, HALF * (f + 1))
 
-        w4_bf = sb("w4bf", [P, PACK * N], BF16)
+        early = [h_banks(2 * c, CH) for c in range(2)]
+        d_banks = [bank(PACK + t, [P, HALF]) for t in range(PACK)]
+        for c in range(2):
+            h_pass(early[c], 0, CH * c, CH, 0)
+        for t in range(PACK):
+            d_pass(d_banks, 0, t, 0)
+        th_early = sb("th_early", [P, 2, 2, CH, 2], F32, "w2_raw")
+        for c in range(2):
+            h_pass(early[c], 0, CH * c, CH, 1)
+            th[0, CH * c] = th_early[:, c]
+            h_tanh(early[c], 0, CH * c)
+            h_gain(0, CH * c, CH)
+        for t in range(PACK):
+            d_pass(d_banks, 0, t, 1)
+        quantize_w1(0, 1)
+        h_quantize(0, 0, HALF, "w1bf01")
+
+        w4d_bf = sb("w4d_bf", [P, PACK * (N + HALF)], BF16)
         nc.vector.tensor_copy(
-            w4_bf[:].rearrange("p (c i t) -> p c t i", i=PACK, t=PACK),
+            w4d_bf[:, 0 : PACK * N].rearrange("p (c i t) -> p c t i", i=PACK, t=PACK),
             w4_raw[:].rearrange("p t (c i) -> p c t i", i=PACK),
         )
-        w4c = sb("w4c", [P, N], U32)
-        w4s = sb("w4s", [P, N], U8)
-        quantize(w4c, w4s, w4_bf, 0, N)
+        sig0 = sb("sig0", [P, PACK, HALF], F32)
+        d_sigmoid(d_banks, sig0[:])
+        d_gain(w4d_bf[:, PACK * N : PACK * (N + HALF)], sig0[:])
+        cast_w1(1, 1, "w2_raw")
+        quantize_w1(1, 1)
+        w4c, w4s = quantize("w4d", w4d_bf[:], "w2_raw")
+        d_banks = [bank(t, [P, HALF]) for t in range(PACK)]
+        for t in range(PACK):
+            for a in range(passes):
+                d_pass(d_banks, 1, t, a)
+        sig1 = sb("sig1", [P, PACK, HALF], F32, "raw11")
+        d_sigmoid(d_banks, sig1[:])
+        d_gain(late_bf[:, 0 : PACK * HALF], sig1[:])
+        d_q = {0: (w4c, w4s, N)}
+
+        last = S - CH
+        def h_sums(first, b, c0, width):
+            banks = h_banks(first, width)
+            for a in range(passes):
+                h_pass(banks, b, c0, width, a)
+            return banks
 
         out_v = out.rearrange("(i p) j -> p i j", p=P)
 
-        def y_chunk(c):
-            cols = slice(CH * c, CH * (c + 1))
-            bank = bank_tile(FIRST_BANKS + c % (BANKS - FIRST_BANKS), [P, N // P, CH])
+        def h_part(banks, b, c0, width, per):
+            codes, scales, at = h_q[b, c0]
             for i in range(N // P):
-                rows = slice(P * i, P * (i + 1))
                 nc.tensor.matmul_mx(
-                    out=bank[:, i, :],
-                    lhsT=w4c[:, rows].bitcast(FP8X4),
-                    lhsT_scale=w4s[:, rows],
-                    rhs=d_codes[:, cols].bitcast(FP8X4),
-                    rhs_scale=d_scales[:, cols],
-                    start=(i == 0),
+                    out=banks[i // per][:, i % per, :],
+                    lhsT=w3c[:, b, 2 * P * i : 2 * P * (i + 1)].bitcast(FP4X4),
+                    lhsT_scale=w3s[:, b, P * i : P * (i + 1)],
+                    rhs=codes[:, at : at + width].bitcast(FP8X4),
+                    rhs_scale=scales[:, at : at + width],
+                    start=False,
+                    stop=(b == blocks - 1 and i % per == per - 1),
+                )
+
+        def y_open(indices, c0, width, per):
+            banks = [bank(index, [P, per, width]) for index in indices]
+            codes, scales, base = d_q[c0 // HALF]
+            at = base + c0 % HALF
+            for i in range(N // P):
+                nc.tensor.matmul_mx(
+                    out=banks[i // per][:, i % per, :],
+                    lhsT=w4c[:, P * i : P * (i + 1)].bitcast(FP8X4),
+                    lhsT_scale=w4s[:, P * i : P * (i + 1)],
+                    rhs=codes[:, at : at + width].bitcast(FP8X4),
+                    rhs_scale=scales[:, at : at + width],
+                    start=(i % per == 0),
                     stop=False,
                 )
-            for b in range(blocks):
-                for i in range(N // P):
-                    nc.tensor.matmul_mx(
-                        out=bank[:, i, :],
-                        lhsT=w3c[:, b, 2 * P * i : 2 * P * (i + 1)].bitcast(FP4X4),
-                        lhsT_scale=w3s[:, b, P * i : P * (i + 1)],
-                        rhs=h_codes[b][:, cols].bitcast(FP8X4),
-                        rhs_scale=h_scales[b][:, cols],
-                        start=False,
-                        stop=(b == blocks - 1 and i == N // P - 1),
-                    )
-            res = sb("res%d" % c, [P, N // P, CH], F32)
-            step = N // P // (2 if c == chunks - 1 else 1)
-            for i in range(0, N // P, step):
-                nc.scalar.activation(res[:, i : i + step], bank[:, i : i + step], ACT.Gelu_apprx_tanh)
-                nc.sync.dma_start(out_v[:, i : i + step, cols], res[:, i : i + step])
+            return banks
 
-        turns = list(range(FIRST_BANKS - 1, FIRST_BANKS - 1 + chunks + per_half))
+        def y_close(banks, c0, width, per):
+            h_part(banks, 1, c0, width, per)
+            for u in range(len(banks)):
+                res = sb("res%d_%d" % (c0, u), [P, per, width], F32)
+                nc.scalar.activation(res[:], banks[u][:], ACT.Gelu_apprx_tanh)
+                nc.sync.dma_start(out_v[:, per * u : per * (u + 1), c0 : c0 + width], res[:])
 
-        def h_chunk(b, c, th):
-            bank = bank_tile(turns.pop(0) % FIRST_BANKS, [P, PACK, CH])
-            for a in range(passes):
-                h_pass(bank, b, c, a)
-            h_finish(bank, b, c, th)
+        waiting = [h_sums(PACK + 2 * c, 0, HALF + CH * c, CH) for c in range(2)]
+        th_late = sb("th_late", [P, 2, 2, CH, 2], F32, "sig0")
+        for c in range(2):
+            th[0, HALF + CH * c] = th_late[:, c]
+            h_tanh(waiting[c], 0, HALF + CH * c)
+        for c in range(3):
+            h_first(2 * c, 1, CH * c, CH)
+        first = y_open((0, 1), 0, CH, 2)
+        h_part(first, 0, 0, CH, 2)
+        for c in range(2):
+            h_first(6 + c, 1, last + P * c, P)
 
-        th_second = sb("th_second", [P, per_half, CH, PACK], F32)
-        for c in range(chunks + 1):
-            if per_half <= c < chunks:
-                h_chunk(0, c, th_second[:, c - per_half])
-            if c > 0:
-                quantize(h_codes[1], h_scales[1], h_bf[1], CH * (c - 1), CH * c)
-            if c < chunks:
-                h_chunk(1, c, sb("th%d" % c, [P, CH, PACK], F32)[:])
-            if per_half <= c < chunks:
-                quantize(h_codes[0], h_scales[0], h_bf[0], CH * c, CH * (c + 1))
-            if c > 0:
-                y_chunk(c - 1)
+        h_gain(1, 0, CH)
+        d_q[1] = quantize("dq", late_bf[:, 0 : PACK * HALF], "th1_0") + (0,)
+        h_gain(1, CH, CH)
+        h_quantize(1, 0, CH, "th1_%d" % CH)
+        h_gain(0, 2 * CH, CH)
+        h_quantize(1, CH, CH, None)
+        h_gain(1, 2 * CH, CH)
+        h_quantize(0, 2 * CH, CH, "th1_%d" % (2 * CH))
+        h_gain(0, last, CH)
+        h_quantize(1, 2 * CH, CH, "sig0")
+        h_quantize(0, last, CH, None)
+        h_gain(1, last, P)
+        h_gain(1, last + P, P)
+        h_quantize(1, last, P, "th1_%d" % (last + P))
+        h_quantize(1, last + P, P, None)
+
+        second = y_open((2, 3), CH, CH, 2)
+        h_part(second, 0, CH, CH, 2)
+        y_close(first, 0, CH, 2)
+        y_close(second, CH, CH, 2)
+        late = [(2 * CH, CH, 2), (last, P, 4), (last + P, P, 2)]
+        opened = [y_open(indices, *part) for indices, part in zip([(0, 1), (4,), (5, 6)], late)]
+        h_part(opened[0], 0, *late[0])
+        y_close(opened[0], *late[0])
+        for banks, part in zip(opened[1:], late[1:]):
+            h_part(banks, 0, *part)
+        for banks, part in zip(opened[1:], late[1:]):
+            y_close(banks, *part)

@@ -15,6 +15,7 @@ FP8X4 = mybir.dt.float8_e4m3fn_x4
 FP4X4 = mybir.dt.float4_e2m1fn_x4
 ACT = mybir.ActivationFunctionType
 MULT = mybir.AluOpType.mult
+ADD = mybir.AluOpType.add
 
 P = 128
 PACK = 4
@@ -108,11 +109,23 @@ def tile_list_unfollow_forecast_features_kernel(
         w1_bf = {}
         w1_q = {}
 
-        def cast_w1(a, b, tag=None):
-            grouped = sb("w1bf%d%d" % (a, b), [P, PACK * KP], BF16, tag)
+        def cast_w1(a, b):
+            grouped = sb("w1bf%d%d" % (a, b), [P, PACK * KP], BF16)
             nc.scalar.copy(
                 grouped[:].rearrange("p (t m j) -> p m j t", t=PACK, j=PACK),
                 w1_raw[a, b][:].rearrange("p j (m t) -> p m j t", t=PACK),
+            )
+            w1_bf[a, b] = grouped
+
+        def cast_w1_aside(a, b):
+            grouped = sb("w1bf%d%d" % (a, b), [P, PACK * KP], BF16)
+            nc.gpsimd.tensor_scalar(
+                grouped[:].rearrange("p (t m j) -> p t m j", t=PACK, j=PACK),
+                w1_raw[a, b][:].rearrange("p j (m t) -> p t m j", t=PACK),
+                1.0,
+                0.0,
+                MULT,
+                ADD,
             )
             w1_bf[a, b] = grouped
 
@@ -135,9 +148,9 @@ def tile_list_unfollow_forecast_features_kernel(
         gather(picked[:, 1, :], swin, list2, 0, S)
         move_scales(0)
         load_tab(1)
-        load_w1(0, 1)
-        move_scales(1)
         nc.sync.dma_start(w2_raw[:], w2_words.rearrange("a p c i -> p a (c i)").bitcast(I32))
+        move_scales(1)
+        load_w1(0, 1)
         load_w1(1, 1)
         nc.sync.dma_start(b2[:], bias2.rearrange("(p t) -> p t", t=PACK))
         nc.sync.dma_start(g2[:], gain2.rearrange("(p t) -> p t", t=PACK))
@@ -161,7 +174,7 @@ def tile_list_unfollow_forecast_features_kernel(
         gather_v2(0, "w1bf00")
         cast_w1(1, 0)
         quantize_w1(1, 0)
-        cast_w1(0, 1)
+        cast_w1_aside(0, 1)
         nc.scalar.copy(
             w2c[:].rearrange("p a (t m) -> p a m t", t=PACK),
             w2_raw[:].bitcast(U32).rearrange("p a (m t) -> p a m t", t=PACK),
@@ -225,6 +238,8 @@ def tile_list_unfollow_forecast_features_kernel(
             for c in range(c0, c0 + width, P):
                 h_q[b, c] = (codes, scales, c - c0)
 
+        d_q = {}
+
         def d_pass(banks, f, t, a):
             nc.tensor.matmul_mx(
                 out=banks[t][:],
@@ -248,50 +263,6 @@ def tile_list_unfollow_forecast_features_kernel(
                 MULT,
             )
 
-        early = [h_banks(2 * c, CH) for c in range(2)]
-        d_banks = [bank(PACK + t, [P, HALF]) for t in range(PACK)]
-        for c in range(2):
-            h_pass(early[c], 0, CH * c, CH, 0)
-        for t in range(PACK):
-            d_pass(d_banks, 0, t, 0)
-        th_early = sb("th_early", [P, 2, 2, CH, 2], F32, "w2_raw")
-        for c in range(2):
-            h_pass(early[c], 0, CH * c, CH, 1)
-            th[0, CH * c] = th_early[:, c]
-            h_tanh(early[c], 0, CH * c)
-            h_gain(0, CH * c, CH)
-        for t in range(PACK):
-            d_pass(d_banks, 0, t, 1)
-        quantize_w1(0, 1)
-        h_quantize(0, 0, HALF, "w1bf01")
-
-        w4d_bf = sb("w4d_bf", [P, PACK * (N + HALF)], BF16)
-        nc.vector.tensor_copy(
-            w4d_bf[:, 0 : PACK * N].rearrange("p (c i t) -> p c t i", i=PACK, t=PACK),
-            w4_raw[:].rearrange("p t (c i) -> p c t i", i=PACK),
-        )
-        sig0 = sb("sig0", [P, PACK, HALF], F32)
-        d_sigmoid(d_banks, sig0[:])
-        d_gain(w4d_bf[:, PACK * N : PACK * (N + HALF)], sig0[:])
-        cast_w1(1, 1, "w2_raw")
-        quantize_w1(1, 1)
-        w4c, w4s = quantize("w4d", w4d_bf[:], "w2_raw")
-        d_banks = [bank(t, [P, HALF]) for t in range(PACK)]
-        for t in range(PACK):
-            for a in range(passes):
-                d_pass(d_banks, 1, t, a)
-        sig1 = sb("sig1", [P, PACK, HALF], F32, "raw11")
-        d_sigmoid(d_banks, sig1[:])
-        d_gain(late_bf[:, 0 : PACK * HALF], sig1[:])
-        d_q = {0: (w4c, w4s, N)}
-
-        last = S - CH
-        def h_sums(first, b, c0, width):
-            banks = h_banks(first, width)
-            for a in range(passes):
-                h_pass(banks, b, c0, width, a)
-            return banks
-
         out_v = out.rearrange("(i p) j -> p i j", p=P)
 
         def h_part(banks, b, c0, width, per):
@@ -314,8 +285,8 @@ def tile_list_unfollow_forecast_features_kernel(
             for i in range(N // P):
                 nc.tensor.matmul_mx(
                     out=banks[i // per][:, i % per, :],
-                    lhsT=w4c[:, P * i : P * (i + 1)].bitcast(FP8X4),
-                    lhsT_scale=w4s[:, P * i : P * (i + 1)],
+                    lhsT=d_q[0][0][:, P * i : P * (i + 1)].bitcast(FP8X4),
+                    lhsT_scale=d_q[0][1][:, P * i : P * (i + 1)],
                     rhs=codes[:, at : at + width].bitcast(FP8X4),
                     rhs_scale=scales[:, at : at + width],
                     start=(i % per == 0),
@@ -330,43 +301,75 @@ def tile_list_unfollow_forecast_features_kernel(
                 nc.scalar.activation(res[:], banks[u][:], ACT.Gelu_apprx_tanh)
                 nc.sync.dma_start(out_v[:, per * u : per * (u + 1), c0 : c0 + width], res[:])
 
-        waiting = [h_sums(PACK + 2 * c, 0, HALF + CH * c, CH) for c in range(2)]
-        th_late = sb("th_late", [P, 2, 2, CH, 2], F32, "sig0")
+        early = [h_banks(2 * c, CH) for c in range(2)]
+        d_banks = [bank(PACK + t, [P, HALF]) for t in range(PACK)]
         for c in range(2):
-            th[0, HALF + CH * c] = th_late[:, c]
-            h_tanh(waiting[c], 0, HALF + CH * c)
-        for c in range(3):
+            h_pass(early[c], 0, CH * c, CH, 0)
+        for t in range(PACK):
+            d_pass(d_banks, 0, t, 0)
+        th_early = sb("th_early", [P, 2, 2, CH, 2], F32)
+        for c in range(2):
+            h_pass(early[c], 0, CH * c, CH, 1)
+            th[0, CH * c] = th_early[:, c]
+            h_tanh(early[c], 0, CH * c)
+            h_gain(0, CH * c, CH)
+        for t in range(PACK):
+            d_pass(d_banks, 0, t, 1)
+        quantize_w1(0, 1)
+        h_quantize(0, 0, HALF, "w1bf01")
+        cast_w1(1, 1)
+
+        quantize_w1(1, 1)
+        w4d_bf = sb("w4d_bf", [P, PACK * (N + HALF)], BF16)
+        nc.vector.tensor_copy(
+            w4d_bf[:, 0 : PACK * N].rearrange("p (c i t) -> p c t i", i=PACK, t=PACK),
+            w4_raw[:].rearrange("p t (c i) -> p c t i", i=PACK),
+        )
+        sig0 = sb("sig0", [P, PACK, HALF], F32, "raw11")
+        d_sigmoid(d_banks, sig0[:])
+        d_gain(w4d_bf[:, PACK * N : PACK * (N + HALF)], sig0[:])
+
+        for c in range(2):
             h_first(2 * c, 1, CH * c, CH)
-        first = y_open((0, 1), 0, CH, 2)
-        h_part(first, 0, 0, CH, 2)
+        d_banks = [bank(PACK + t, [P, HALF]) for t in range(PACK)]
+        for t in range(PACK):
+            for a in range(passes):
+                d_pass(d_banks, 1, t, a)
+        sig1 = sb("sig1", [P, PACK, HALF], F32, "w1bf11")
+        d_sigmoid(d_banks, sig1[:])
+        last = S - CH
+        h_first(0, 0, HALF, CH)
+        h_first(4, 1, HALF, CH)
+        h_first(2, 0, last, CH)
         for c in range(2):
             h_first(6 + c, 1, last + P * c, P)
 
         h_gain(1, 0, CH)
-        d_q[1] = quantize("dq", late_bf[:, 0 : PACK * HALF], "th1_0") + (0,)
+        w4c, w4s = quantize("w4d", w4d_bf[:], "th1_0")
+        d_q[0] = (w4c, w4s, N)
         h_gain(1, CH, CH)
         h_quantize(1, 0, CH, "th1_%d" % CH)
-        h_gain(0, 2 * CH, CH)
-        h_quantize(1, CH, CH, None)
-        h_gain(1, 2 * CH, CH)
-        h_quantize(0, 2 * CH, CH, "th1_%d" % (2 * CH))
+        d_gain(late_bf[:, 0 : PACK * HALF], sig1[:])
+        h_quantize(1, CH, CH, "w1bf11")
+        h_gain(0, HALF, CH)
+        d_q[1] = quantize("dq", late_bf[:, 0 : PACK * HALF], "th0_%d" % HALF) + (0,)
+        h_gain(1, HALF, CH)
+        h_quantize(0, HALF, CH, "th1_%d" % HALF)
         h_gain(0, last, CH)
-        h_quantize(1, 2 * CH, CH, "sig0")
-        h_quantize(0, last, CH, None)
+        h_quantize(1, HALF, CH, "th0_%d" % last)
         h_gain(1, last, P)
+        h_quantize(0, last, CH, "th1_%d" % last)
+        h_quantize(1, last, P, None)
         h_gain(1, last + P, P)
-        h_quantize(1, last, P, "th1_%d" % (last + P))
         h_quantize(1, last + P, P, None)
 
-        second = y_open((2, 3), CH, CH, 2)
-        h_part(second, 0, CH, CH, 2)
-        y_close(first, 0, CH, 2)
-        y_close(second, CH, CH, 2)
-        late = [(2 * CH, CH, 2), (last, P, 4), (last + P, P, 2)]
-        opened = [y_open(indices, *part) for indices, part in zip([(0, 1), (4,), (5, 6)], late)]
-        h_part(opened[0], 0, *late[0])
-        y_close(opened[0], *late[0])
-        for banks, part in zip(opened[1:], late[1:]):
-            h_part(banks, 0, *part)
-        for banks, part in zip(opened[1:], late[1:]):
-            y_close(banks, *part)
+        parts = [((0, 1), 0, CH, 2), ((4, 5), CH, CH, 2), ((0, 1), HALF, CH, 2)]
+        for indices, c0, width, per in parts:
+            banks = y_open(indices, c0, width, per)
+            h_part(banks, 0, c0, width, per)
+            y_close(banks, c0, width, per)
+        late = [((4,), last, P, 4), ((5, 2), last + P, P, 2)]
+        opened = [y_open(*part) for part in late]
+        for banks, part in zip(opened, late):
+            h_part(banks, 0, *part[1:])
+            y_close(banks, *part[1:])

@@ -15,7 +15,6 @@ FP8X4 = mybir.dt.float8_e4m3fn_x4
 FP4X4 = mybir.dt.float4_e2m1fn_x4
 ACT = mybir.ActivationFunctionType
 MULT = mybir.AluOpType.mult
-ADD = mybir.AluOpType.add
 
 P = 128
 PACK = 4
@@ -109,23 +108,11 @@ def tile_list_unfollow_forecast_features_kernel(
         w1_bf = {}
         w1_q = {}
 
-        def cast_w1(a, b):
-            grouped = sb("w1bf%d%d" % (a, b), [P, PACK * KP], BF16)
+        def cast_w1(a, b, tag=None):
+            grouped = sb("w1bf%d%d" % (a, b), [P, PACK * KP], BF16, tag)
             nc.scalar.copy(
                 grouped[:].rearrange("p (t m j) -> p m j t", t=PACK, j=PACK),
                 w1_raw[a, b][:].rearrange("p j (m t) -> p m j t", t=PACK),
-            )
-            w1_bf[a, b] = grouped
-
-        def cast_w1_aside(a, b):
-            grouped = sb("w1bf%d%d" % (a, b), [P, PACK * KP], BF16)
-            nc.gpsimd.tensor_scalar(
-                grouped[:].rearrange("p (t m j) -> p t m j", t=PACK, j=PACK),
-                w1_raw[a, b][:].rearrange("p j (m t) -> p t m j", t=PACK),
-                1.0,
-                0.0,
-                MULT,
-                ADD,
             )
             w1_bf[a, b] = grouped
 
@@ -147,14 +134,14 @@ def tile_list_unfollow_forecast_features_kernel(
         gather(picked[:, 0, :], swin, list1, 0, S)
         gather(picked[:, 1, :], swin, list2, 0, S)
         move_scales(0)
-        load_tab(1)
         nc.sync.dma_start(w2_raw[:], w2_words.rearrange("a p c i -> p a (c i)").bitcast(I32))
+        load_tab(1)
         move_scales(1)
         load_w1(0, 1)
-        load_w1(1, 1)
         nc.sync.dma_start(b2[:], bias2.rearrange("(p t) -> p t", t=PACK))
         nc.sync.dma_start(g2[:], gain2.rearrange("(p t) -> p t", t=PACK))
         nc.sync.dma_start(w4_raw[:], w4.rearrange("(p j) n -> p j n", j=PACK))
+        load_w1(1, 1)
         nc.sync.dma_start(w3c[:].bitcast(I32), w3_words.rearrange("a p n -> p a n").bitcast(I32))
         load_scale_rows(w3s, w3_scales)
 
@@ -174,7 +161,6 @@ def tile_list_unfollow_forecast_features_kernel(
         gather_v2(0, "w1bf00")
         cast_w1(1, 0)
         quantize_w1(1, 0)
-        cast_w1_aside(0, 1)
         nc.scalar.copy(
             w2c[:].rearrange("p a (t m) -> p a m t", t=PACK),
             w2_raw[:].bitcast(U32).rearrange("p a (m t) -> p a m t", t=PACK),
@@ -211,16 +197,20 @@ def tile_list_unfollow_forecast_features_kernel(
 
         th = {}
 
-        def h_tanh(banks, b, c0):
+        def h_tanh(banks, b, c0, dst=None):
+            shape = [P, len(banks), banks[0].shape[2], banks[0].shape[1]]
+            th[b, c0] = sb("th%d_%d" % (b, c0), shape, F32)[:] if dst is None else dst
             for u in range(len(banks)):
                 nc.scalar.activation(th[b, c0][:, u], banks[u][:].rearrange("p e n -> p n e"), ACT.Tanh)
 
-        def h_first(first, b, c0, width):
+        def h_sums(first, b, c0, width):
             banks = h_banks(first, width)
             for a in range(passes):
                 h_pass(banks, b, c0, width, a)
-            th[b, c0] = sb("th%d_%d" % (b, c0), [P, len(banks), width, PACK // len(banks)], F32)[:]
-            h_tanh(banks, b, c0)
+            return banks
+
+        def h_first(first, b, c0, width):
+            h_tanh(h_sums(first, b, c0, width), b, c0)
 
         def h_gain(b, c0, width):
             per = BANK // width
@@ -307,68 +297,69 @@ def tile_list_unfollow_forecast_features_kernel(
             h_pass(early[c], 0, CH * c, CH, 0)
         for t in range(PACK):
             d_pass(d_banks, 0, t, 0)
-        th_early = sb("th_early", [P, 2, 2, CH, 2], F32)
         for c in range(2):
             h_pass(early[c], 0, CH * c, CH, 1)
-            th[0, CH * c] = th_early[:, c]
             h_tanh(early[c], 0, CH * c)
             h_gain(0, CH * c, CH)
         for t in range(PACK):
             d_pass(d_banks, 0, t, 1)
+        cast_w1(0, 1)
         quantize_w1(0, 1)
         h_quantize(0, 0, HALF, "w1bf01")
-        cast_w1(1, 1)
 
-        quantize_w1(1, 1)
         w4d_bf = sb("w4d_bf", [P, PACK * (N + HALF)], BF16)
         nc.vector.tensor_copy(
             w4d_bf[:, 0 : PACK * N].rearrange("p (c i t) -> p c t i", i=PACK, t=PACK),
             w4_raw[:].rearrange("p t (c i) -> p c t i", i=PACK),
         )
-        sig0 = sb("sig0", [P, PACK, HALF], F32, "raw11")
+        sig0 = sb("sig0", [P, PACK, HALF], F32)
         d_sigmoid(d_banks, sig0[:])
         d_gain(w4d_bf[:, PACK * N : PACK * (N + HALF)], sig0[:])
-
-        for c in range(2):
-            h_first(2 * c, 1, CH * c, CH)
-        d_banks = [bank(PACK + t, [P, HALF]) for t in range(PACK)]
+        d_banks = [bank(t, [P, HALF]) for t in range(PACK)]
         for t in range(PACK):
             for a in range(passes):
                 d_pass(d_banks, 1, t, a)
-        sig1 = sb("sig1", [P, PACK, HALF], F32, "w1bf11")
+        waiting = [h_sums(PACK + 2 * c, 0, HALF + CH * c, CH) for c in range(2)]
+        cast_w1(1, 1, "th0_%d" % CH)
+        quantize_w1(1, 1)
+        d_q[0] = quantize("w4d", w4d_bf[:], "th0_%d" % CH) + (N,)
+        sig1 = sb("sig1", [P, PACK, HALF], F32, "raw11")
         d_sigmoid(d_banks, sig1[:])
+        d_gain(late_bf[:, 0 : PACK * HALF], sig1[:])
+
         last = S - CH
-        h_first(0, 0, HALF, CH)
-        h_first(4, 1, HALF, CH)
-        h_first(2, 0, last, CH)
+        th_late = sb("th_late", [P, 2, 2, CH, 2], F32, "w4d_bf")
+        for c in range(2):
+            h_tanh(waiting[c], 0, HALF + CH * c, th_late[:, c])
+        for c in range(3):
+            h_first(2 * c, 1, CH * c, CH)
+        first = y_open((0, 1), 0, CH, 2)
+        h_part(first, 0, 0, CH, 2)
         for c in range(2):
             h_first(6 + c, 1, last + P * c, P)
 
+        h_gain(0, HALF, CH)
         h_gain(1, 0, CH)
-        w4c, w4s = quantize("w4d", w4d_bf[:], "th1_0")
-        d_q[0] = (w4c, w4s, N)
         h_gain(1, CH, CH)
         h_quantize(1, 0, CH, "th1_%d" % CH)
-        d_gain(late_bf[:, 0 : PACK * HALF], sig1[:])
-        h_quantize(1, CH, CH, "w1bf11")
-        h_gain(0, HALF, CH)
-        d_q[1] = quantize("dq", late_bf[:, 0 : PACK * HALF], "th0_%d" % HALF) + (0,)
+        d_q[1] = quantize("dq", late_bf[:, 0 : PACK * HALF], "th1_0") + (0,)
+        h_quantize(1, CH, CH, None)
         h_gain(1, HALF, CH)
         h_quantize(0, HALF, CH, "th1_%d" % HALF)
         h_gain(0, last, CH)
-        h_quantize(1, HALF, CH, "th0_%d" % last)
+        h_quantize(1, HALF, CH, "w4d_bf")
         h_gain(1, last, P)
         h_quantize(0, last, CH, "th1_%d" % last)
         h_quantize(1, last, P, None)
         h_gain(1, last + P, P)
         h_quantize(1, last + P, P, None)
 
-        parts = [((0, 1), 0, CH, 2), ((4, 5), CH, CH, 2), ((0, 1), HALF, CH, 2)]
-        for indices, c0, width, per in parts:
-            banks = y_open(indices, c0, width, per)
-            h_part(banks, 0, c0, width, per)
-            y_close(banks, c0, width, per)
-        late = [((4,), last, P, 4), ((5, 2), last + P, P, 2)]
+        y_close(first, 0, CH, 2)
+        for c in range(1, 3):
+            banks = y_open((2 * c, 2 * c + 1), CH * c, CH, 2)
+            h_part(banks, 0, CH * c, CH, 2)
+            y_close(banks, CH * c, CH, 2)
+        late = [((6,), last, P, 4), ((7, 0, 1, 2), last + P, P, 1)]
         opened = [y_open(*part) for part in late]
         for banks, part in zip(opened, late):
             h_part(banks, 0, *part[1:])

@@ -38,6 +38,7 @@ def tile_list_unfollow_forecast_features_kernel(
 
     with ExitStack() as ctx:
         keep = ctx.enter_context(tc.tile_pool(name="keep", bufs=1))
+        placed = ctx.enter_context(tc.tile_pool(name="placed", bufs=1))
         psum = ctx.enter_context(tc.psum_pool(name="psum", bufs=1))
 
         def sb(name, shape, dtype, tag=None):
@@ -87,7 +88,10 @@ def tile_list_unfollow_forecast_features_kernel(
         w1_raw = {}
 
         def load_w1(a, b):
-            raw = sb("raw%d%d" % (a, b), [P, PACK, KP], F32)
+            if (a, b) == (1, 1):
+                raw = placed.tile([P, PACK, KP], F32, name="raw11", align_bytes=64, offset=0)
+            else:
+                raw = sb("raw%d%d" % (a, b), [P, PACK, KP], F32)
             nc.sync.dma_start(raw[:], w1[KP * a : KP * (a + 1), KP * b : KP * (b + 1)].rearrange("(p j) c -> p j c", j=PACK))
             w1_raw[a, b] = raw
 
@@ -98,10 +102,10 @@ def tile_list_unfollow_forecast_features_kernel(
                     planes[a][QUAD * q : QUAD * q + SROWS].bitcast(I32), picked[row : row + SROWS].bitcast(I32)
                 )
 
-        def quantize(name, values, tag=None):
+        def quantize(name, values, tag=None, scales=None):
             width = values.shape[1] // PACK
             codes = sb(name + "c", [P, width], U32, tag)
-            scales = sb(name + "s", [P, width], U8)
+            scales = sb(name + "s", [P, width], U8) if scales is None else scales
             nc.vector.quantize_mx(out=codes[:].bitcast(FP8X4), scales=scales[:], in_=values)
             return codes, scales
 
@@ -134,8 +138,8 @@ def tile_list_unfollow_forecast_features_kernel(
         gather(picked[:, 0, :], swin, list1, 0, S)
         gather(picked[:, 1, :], swin, list2, 0, S)
         move_scales(0)
-        nc.sync.dma_start(w2_raw[:], w2_words.rearrange("a p c i -> p a (c i)").bitcast(I32))
         load_tab(1)
+        nc.sync.dma_start(w2_raw[:], w2_words.rearrange("a p c i -> p a (c i)").bitcast(I32))
         move_scales(1)
         load_w1(0, 1)
         nc.sync.dma_start(b2[:], bias2.rearrange("(p t) -> p t", t=PACK))
@@ -148,9 +152,9 @@ def tile_list_unfollow_forecast_features_kernel(
         v1 = [sb("v1_%d" % a, [P, S], U16) for a in range(passes)]
         v2 = {}
 
-        def gather_v2(a, tag=None):
-            v2[a] = sb("v2_%d" % a, [P, S], U16, tag)
-            gather(v2[a][:], wwin[a], list2, 0, S)
+        def gather_v2(a, f, tag=None):
+            v2[a, f] = sb("v2_%d%d" % (a, f), [P, HALF], U16, tag)
+            gather(v2[a, f][:], wwin[a], list2, HALF * f, HALF * (f + 1))
 
         gather(v1[0][:], wwin[0], list1, 0, S)
         nc.vector.tensor_copy(
@@ -158,7 +162,7 @@ def tile_list_unfollow_forecast_features_kernel(
         )
         cast_w1(0, 0)
         quantize_w1(0, 0)
-        gather_v2(0, "w1bf00")
+        gather_v2(0, 0, "raw00")
         cast_w1(1, 0)
         quantize_w1(1, 0)
         nc.scalar.copy(
@@ -167,13 +171,19 @@ def tile_list_unfollow_forecast_features_kernel(
         )
         for f in range(halves):
             gather(v1[1][:, HALF * f : HALF * (f + 1)], wwin[1], list1, HALF * f, HALF * (f + 1))
-        gather_v2(1)
+        for f in range(halves):
+            gather_v2(1, f)
+        gather_v2(0, 1, "picked")
 
         early_bf = sb("early_bf", [P, PACK * HALF], BF16)
         late_bf = sb("late_bf", [P, PACK * S], BF16)
         h1_bf = sb("h1_bf", [P, PACK * S], BF16)
 
+        own_bf = {}
+
         def h_bf(b, c0, width):
+            if (b, c0) in own_bf:
+                return own_bf[b, c0][:]
             tile = h1_bf if b == 1 else early_bf if c0 < HALF else late_bf
             return tile[:, PACK * c0 : PACK * (c0 + width)]
 
@@ -235,7 +245,7 @@ def tile_list_unfollow_forecast_features_kernel(
                 out=banks[t][:],
                 lhsT=w2c[:, a, P * t : P * (t + 1)].bitcast(FP8X4),
                 lhsT_scale=w2s[:, a, P * t : P * (t + 1)],
-                rhs=v2[a][:, HALF * f : HALF * (f + 1)].bitcast(FP4X4),
+                rhs=v2[a, f][:].bitcast(FP4X4),
                 rhs_scale=planes[a][:, 1, HALF * f : HALF * (f + 1)],
                 start=(a == 0),
                 stop=(a == passes - 1),
@@ -255,112 +265,117 @@ def tile_list_unfollow_forecast_features_kernel(
 
         out_v = out.rearrange("(i p) j -> p i j", p=P)
 
-        def h_part(banks, b, c0, width, per):
-            codes, scales, at = h_q[b, c0]
+        def y_banks(indices, width):
+            return [bank(index, [P, N // P // len(indices), width]) for index in indices]
+
+        def y_passes(banks, c0, source, start=False, stop=False):
+            per, width = banks[0].shape[1:]
+            codes, scales, at = d_q[c0 // HALF] if source == "d" else h_q[source, c0]
+            at = at + c0 % HALF if source == "d" else at
             for i in range(N // P):
+                rows = slice(P * i, P * (i + 1))
+                if source == "d":
+                    weights, weight_scales = d_q[0][0][:, rows].bitcast(FP8X4), d_q[0][1][:, rows]
+                else:
+                    weights, weight_scales = w3c[:, source, 2 * P * i : 2 * P * (i + 1)].bitcast(FP4X4), w3s[:, source, rows]
                 nc.tensor.matmul_mx(
                     out=banks[i // per][:, i % per, :],
-                    lhsT=w3c[:, b, 2 * P * i : 2 * P * (i + 1)].bitcast(FP4X4),
-                    lhsT_scale=w3s[:, b, P * i : P * (i + 1)],
+                    lhsT=weights,
+                    lhsT_scale=weight_scales,
                     rhs=codes[:, at : at + width].bitcast(FP8X4),
                     rhs_scale=scales[:, at : at + width],
-                    start=False,
-                    stop=(b == blocks - 1 and i % per == per - 1),
+                    start=(start and i % per == 0),
+                    stop=(stop and i % per == per - 1),
                 )
 
-        def y_open(indices, c0, width, per):
-            banks = [bank(index, [P, per, width]) for index in indices]
-            codes, scales, base = d_q[c0 // HALF]
-            at = base + c0 % HALF
-            for i in range(N // P):
-                nc.tensor.matmul_mx(
-                    out=banks[i // per][:, i % per, :],
-                    lhsT=d_q[0][0][:, P * i : P * (i + 1)].bitcast(FP8X4),
-                    lhsT_scale=d_q[0][1][:, P * i : P * (i + 1)],
-                    rhs=codes[:, at : at + width].bitcast(FP8X4),
-                    rhs_scale=scales[:, at : at + width],
-                    start=(i % per == 0),
-                    stop=False,
-                )
+        def y_open(indices, c0, width):
+            banks = y_banks(indices, width)
+            y_passes(banks, c0, "d", start=True)
             return banks
 
-        def y_close(banks, c0, width, per):
-            h_part(banks, 1, c0, width, per)
+        def y_close(banks, c0, source):
+            y_passes(banks, c0, source, stop=True)
+            per, width = banks[0].shape[1:]
             for u in range(len(banks)):
                 res = sb("res%d_%d" % (c0, u), [P, per, width], F32)
                 nc.scalar.activation(res[:], banks[u][:], ACT.Gelu_apprx_tanh)
                 nc.sync.dma_start(out_v[:, per * u : per * (u + 1), c0 : c0 + width], res[:])
 
-        early = [h_banks(2 * c, CH) for c in range(2)]
-        d_banks = [bank(PACK + t, [P, HALF]) for t in range(PACK)]
-        for c in range(2):
-            h_pass(early[c], 0, CH * c, CH, 0)
-        for t in range(PACK):
-            d_pass(d_banks, 0, t, 0)
-        for c in range(2):
-            h_pass(early[c], 0, CH * c, CH, 1)
+        early = [h_banks(2 * c, CH) for c in range(4)]
+        for a in range(passes):
+            for c in range(4):
+                h_pass(early[c], 0, CH * c, CH, a)
+        for c in range(4):
             h_tanh(early[c], 0, CH * c)
-            h_gain(0, CH * c, CH)
-        for t in range(PACK):
-            d_pass(d_banks, 0, t, 1)
+        h_gain(0, 0, CH)
+        h_gain(0, CH, CH)
+        h_gain(0, HALF, CH)
+
+        def d_sums(first, f):
+            banks = [bank(first + t, [P, HALF]) for t in range(PACK)]
+            for t in range(PACK):
+                for a in range(passes):
+                    d_pass(banks, f, t, a)
+            return banks
+
+        d_banks = [d_sums(PACK * f, f) for f in range(halves)]
         cast_w1(0, 1)
         quantize_w1(0, 1)
-        h_quantize(0, 0, HALF, "w1bf01")
-
+        h_quantize(0, 0, HALF, "raw01")
         w4d_bf = sb("w4d_bf", [P, PACK * (N + HALF)], BF16)
         nc.vector.tensor_copy(
             w4d_bf[:, 0 : PACK * N].rearrange("p (c i t) -> p c t i", i=PACK, t=PACK),
             w4_raw[:].rearrange("p t (c i) -> p c t i", i=PACK),
         )
+        h_quantize(0, HALF, CH, None)
         sig0 = sb("sig0", [P, PACK, HALF], F32)
-        d_sigmoid(d_banks, sig0[:])
+        d_sigmoid(d_banks[0], sig0[:])
         d_gain(w4d_bf[:, PACK * N : PACK * (N + HALF)], sig0[:])
-        d_banks = [bank(t, [P, HALF]) for t in range(PACK)]
-        for t in range(PACK):
-            for a in range(passes):
-                d_pass(d_banks, 1, t, a)
-        waiting = [h_sums(PACK + 2 * c, 0, HALF + CH * c, CH) for c in range(2)]
-        cast_w1(1, 1, "th0_%d" % CH)
+        ahead = [h_banks(2 * c, CH) for c in range(2)]
+        for c in range(2):
+            h_pass(ahead[c], 1, CH * c, CH, 0)
+        cast_w1(1, 1, "th0_%d" % HALF)
         quantize_w1(1, 1)
-        d_q[0] = quantize("w4d", w4d_bf[:], "th0_%d" % CH) + (N,)
-        sig1 = sb("sig1", [P, PACK, HALF], F32, "raw11")
-        d_sigmoid(d_banks, sig1[:])
+        w4d_scales = placed.tile([P, N + HALF], U8, name="w4d_scales", align_bytes=64, offset=0)
+        d_q[0] = quantize("w4d", w4d_bf[:], None, w4d_scales) + (N,)
+        sig1 = placed.tile([P, PACK, HALF], F32, name="sig1", align_bytes=64, offset=N + HALF)
+        d_sigmoid(d_banks[1], sig1[:])
         d_gain(late_bf[:, 0 : PACK * HALF], sig1[:])
 
         last = S - CH
-        th_late = sb("th_late", [P, 2, 2, CH, 2], F32, "w4d_bf")
         for c in range(2):
-            h_tanh(waiting[c], 0, HALF + CH * c, th_late[:, c])
-        for c in range(3):
-            h_first(2 * c, 1, CH * c, CH)
-        first = y_open((0, 1), 0, CH, 2)
-        h_part(first, 0, 0, CH, 2)
+            h_pass(ahead[c], 1, CH * c, CH, 1)
+            h_tanh(ahead[c], 1, CH * c)
+        h_first(4, 1, HALF, CH)
+        first = y_open((0, 1), 0, CH)
+        y_passes(first, 0, 0)
         for c in range(2):
             h_first(6 + c, 1, last + P * c, P)
 
-        h_gain(0, HALF, CH)
         h_gain(1, 0, CH)
         h_gain(1, CH, CH)
-        h_quantize(1, 0, CH, "th1_%d" % CH)
-        d_q[1] = quantize("dq", late_bf[:, 0 : PACK * HALF], "th1_0") + (0,)
-        h_quantize(1, CH, CH, None)
+        h_quantize(1, 0, CH, None)
+        d_q[1] = quantize("dq", late_bf[:, 0 : PACK * HALF]) + (0,)
         h_gain(1, HALF, CH)
-        h_quantize(0, HALF, CH, "th1_%d" % HALF)
+        h_quantize(1, CH, CH, None)
+        own_bf[0, last] = sb("h0_last", [P, PACK * CH], BF16, "th1_%d" % CH)
         h_gain(0, last, CH)
-        h_quantize(1, HALF, CH, "w4d_bf")
+        h_quantize(1, HALF, CH, None)
         h_gain(1, last, P)
-        h_quantize(0, last, CH, "th1_%d" % last)
+        h_quantize(0, last, CH, None)
         h_quantize(1, last, P, None)
         h_gain(1, last + P, P)
         h_quantize(1, last + P, P, None)
 
-        y_close(first, 0, CH, 2)
-        for c in range(1, 3):
-            banks = y_open((2 * c, 2 * c + 1), CH * c, CH, 2)
-            h_part(banks, 0, CH * c, CH, 2)
-            y_close(banks, CH * c, CH, 2)
-        late = [((6,), last, P, 4), ((7, 0, 1, 2), last + P, P, 1)]
-        opened = [y_open(*part) for part in late]
-        for banks, part in zip(opened, late):
-            h_part(banks, 0, *part[1:])
-            y_close(banks, *part[1:])
+        second = y_open((2, 3), CH, CH)
+        y_passes(second, CH, 0)
+        y_close(first, 0, 1)
+        third = y_open((4, 5), HALF, CH)
+        y_close(second, CH, 1)
+        y_passes(third, HALF, 0)
+        fourth = y_open((6,), last, P)
+        y_close(third, HALF, 1)
+        fifth = y_open((7, 0, 1, 2), last + P, P)
+        for banks, c0 in ((fourth, last), (fifth, last + P)):
+            y_passes(banks, c0, 0)
+            y_close(banks, c0, 1)

@@ -1,6 +1,7 @@
 from contextlib import ExitStack
 
 import concourse.mybir as mybir
+from concourse.masks import make_identity
 
 K, T, S, H, G, N = 1024, 4096, 1024, 1024, 512, 512
 FLOPS = 2 * S * (K * H + K * G + H * N + G * N)
@@ -15,6 +16,7 @@ FP8X4 = mybir.dt.float8_e4m3fn_x4
 FP4X4 = mybir.dt.float4_e2m1fn_x4
 ACT = mybir.ActivationFunctionType
 MULT = mybir.AluOpType.mult
+ADD = mybir.AluOpType.add
 
 P = 128
 PACK = 4
@@ -26,6 +28,8 @@ LIVE = 96
 CH = 256
 HALF = 512
 BANK = 512
+RUN = 32
+GAIN_BANK = 7
 
 
 def tile_list_unfollow_forecast_features_kernel(
@@ -44,12 +48,17 @@ def tile_list_unfollow_forecast_features_kernel(
         def sb(name, shape, dtype, tag=None):
             return keep.tile(shape, dtype, name=name, tag=tag or name, align_bytes=64)
 
+        def at(name, shape, dtype, offset):
+            return placed.tile(shape, dtype, name=name, align_bytes=64, offset=offset)
+
         def bank(index, shape):
             return psum.tile(shape, F32, name="bank%d" % index)
 
+        window_bytes = 2 * T
+
         list1 = keep.tile([P, S // 16], U16, name="list1")
         list2 = keep.tile([P, S // 16], U16, name="list2")
-        wwin = [sb("wwin%d" % a, [P, T], U16) for a in range(passes)]
+        wwin = [at("wwin%d" % a, [P, T], U16, window_bytes * a) for a in range(passes)]
         swin = sb("swin", [P, T], U8)
         picked = sb("picked", [P, 2, S], U8)
         planes = [sb("plane%d" % a, [P, 2, S], U8) for a in range(passes)]
@@ -63,6 +72,7 @@ def tile_list_unfollow_forecast_features_kernel(
         w2s = sb("w2s", [P, passes, G], U8)
         w4_raw = sb("w4_raw", [P, PACK, N], F32)
         w3c = sb("w3c", [P, blocks, 2 * N], U8)
+        ident = sb("ident", [P, P], F32)
 
         nc.vector.memset(swin[0:LIVE].bitcast(I32), 0)
         for a in range(passes):
@@ -80,6 +90,7 @@ def tile_list_unfollow_forecast_features_kernel(
                 )
 
         nc.gpsimd.memset(w2s_raw[:].bitcast(I32), 0)
+        make_identity(nc, ident[:])
         nc.gpsimd.memset(w3s[:].bitcast(I32), 0)
 
         def load_tab(a):
@@ -88,11 +99,8 @@ def tile_list_unfollow_forecast_features_kernel(
         w1_raw = {}
 
         def load_w1(a, b):
-            if (a, b) == (1, 1):
-                raw = placed.tile([P, PACK, KP], F32, name="raw11", align_bytes=64, offset=0)
-            else:
-                raw = sb("raw%d%d" % (a, b), [P, PACK, KP], F32)
-            nc.sync.dma_start(raw[:], w1[KP * a : KP * (a + 1), KP * b : KP * (b + 1)].rearrange("(p j) c -> p j c", j=PACK))
+            raw = sb("raw%d%d" % (a, b), [P, PACK, KP], F32)[:]
+            nc.sync.dma_start(raw, w1[KP * a : KP * (a + 1), KP * b : KP * (b + 1)].rearrange("(p j) c -> p j c", j=PACK))
             w1_raw[a, b] = raw
 
         def move_scales(a):
@@ -102,26 +110,18 @@ def tile_list_unfollow_forecast_features_kernel(
                     planes[a][QUAD * q : QUAD * q + SROWS].bitcast(I32), picked[row : row + SROWS].bitcast(I32)
                 )
 
-        def quantize(name, values, tag=None, scales=None):
+        def quantize(name, values, tag=None):
             width = values.shape[1] // PACK
-            codes = sb(name + "c", [P, width], U32, tag)
-            scales = sb(name + "s", [P, width], U8) if scales is None else scales
+            codes = sb(name + "c", [P, width], U32)
+            scales = sb(name + "s", [P, width], U8, tag)
             nc.vector.quantize_mx(out=codes[:].bitcast(FP8X4), scales=scales[:], in_=values)
             return codes, scales
 
-        w1_bf = {}
-        w1_q = {}
+        def dealt(grouped):
+            return grouped.rearrange("p (t m j) -> p m j t", t=PACK, j=PACK)
 
-        def cast_w1(a, b, tag=None):
-            grouped = sb("w1bf%d%d" % (a, b), [P, PACK * KP], BF16, tag)
-            nc.scalar.copy(
-                grouped[:].rearrange("p (t m j) -> p m j t", t=PACK, j=PACK),
-                w1_raw[a, b][:].rearrange("p j (m t) -> p m j t", t=PACK),
-            )
-            w1_bf[a, b] = grouped
-
-        def quantize_w1(a, b):
-            w1_q[a, b] = quantize("w1q%d%d" % (a, b), w1_bf[a, b][:])
+        def rows_of(a, b):
+            return w1_raw[a, b].rearrange("p j (m t) -> p m j t", t=PACK)
 
         def gather(dst, window, offsets, c0, c1):
             nc.vector.tensor_copy(dst, window[:].indirect(offsets[:, c0 // 16 : c1 // 16]))
@@ -132,6 +132,7 @@ def tile_list_unfollow_forecast_features_kernel(
         load_tab(0)
         load_scale_rows(w2s_raw, w2_scales)
         nc.sync.dma_start(g1[:], gain1.rearrange("(b p t) -> p b t", b=blocks, t=PACK))
+        nc.sync.dma_start(g2[:], gain2.rearrange("(p t) -> p t", t=PACK))
         load_w1(0, 0)
         load_w1(1, 0)
 
@@ -143,11 +144,26 @@ def tile_list_unfollow_forecast_features_kernel(
         move_scales(1)
         load_w1(0, 1)
         nc.sync.dma_start(b2[:], bias2.rearrange("(p t) -> p t", t=PACK))
-        nc.sync.dma_start(g2[:], gain2.rearrange("(p t) -> p t", t=PACK))
-        nc.sync.dma_start(w4_raw[:], w4.rearrange("(p j) n -> p j n", j=PACK))
         load_w1(1, 1)
+        nc.sync.dma_start(w4_raw[:], w4.rearrange("(p j) n -> p j n", j=PACK))
         nc.sync.dma_start(w3c[:].bitcast(I32), w3_words.rearrange("a p n -> p a n").bitcast(I32))
         load_scale_rows(w3s, w3_scales)
+
+        spread = sb("spread", [P, P], F32)
+        nc.scalar.copy(
+            spread[:, 0 : blocks * RUN].rearrange("p (b i t) -> p b i t", b=blocks, t=PACK),
+            g1[:].rearrange("p b (i t) -> p b i t", i=1).to_broadcast([P, blocks, RUN // PACK, PACK]),
+        )
+        nc.scalar.copy(
+            spread[:, blocks * RUN : P].rearrange("p (c t i) -> p c t i", t=PACK, i=PACK),
+            g2[:].rearrange("p (c t i) -> p c t i", c=1, i=1).to_broadcast([P, PACK, PACK, PACK]),
+        )
+        turned_ps = bank(0, [P, P])
+        nc.tensor.transpose(turned_ps[:], spread[:], ident[:])
+        turned = sb("turned", [P, P], F32)
+        nc.scalar.copy(turned[:], turned_ps[:])
+        gains = bank(GAIN_BANK, [P, P])
+        nc.tensor.transpose(gains[:], turned[:], ident[:])
 
         v1 = [sb("v1_%d" % a, [P, S], U16) for a in range(passes)]
         v2 = {}
@@ -156,15 +172,20 @@ def tile_list_unfollow_forecast_features_kernel(
             v2[a, f] = sb("v2_%d%d" % (a, f), [P, HALF], U16, tag)
             gather(v2[a, f][:], wwin[a], list2, HALF * f, HALF * (f + 1))
 
+        w1_q = {}
+
+        def early_w1(a):
+            grouped = sb("w1bf%d" % a, [P, PACK * KP], BF16)
+            nc.scalar.copy(dealt(grouped[:]), rows_of(a, 0))
+            w1_q[a, 0] = quantize("w1q%d" % a, grouped[:]) + (0,)
+
         gather(v1[0][:], wwin[0], list1, 0, S)
         nc.vector.tensor_copy(
             w2s[:].rearrange("p a (t m) -> p a m t", t=PACK), w2s_raw[:].rearrange("p a (m t) -> p a m t", t=PACK)
         )
-        cast_w1(0, 0)
-        quantize_w1(0, 0)
+        early_w1(0)
         gather_v2(0, 0, "raw00")
-        cast_w1(1, 0)
-        quantize_w1(1, 0)
+        early_w1(1)
         nc.scalar.copy(
             w2c[:].rearrange("p a (t m) -> p a m t", t=PACK),
             w2_raw[:].bitcast(U32).rearrange("p a (m t) -> p a m t", t=PACK),
@@ -175,30 +196,24 @@ def tile_list_unfollow_forecast_features_kernel(
             gather_v2(1, f)
         gather_v2(0, 1, "picked")
 
-        early_bf = sb("early_bf", [P, PACK * HALF], BF16)
-        late_bf = sb("late_bf", [P, PACK * S], BF16)
+        line = sb("line", [P, PACK * (S + HALF)], BF16)
         h1_bf = sb("h1_bf", [P, PACK * S], BF16)
 
-        own_bf = {}
-
         def h_bf(b, c0, width):
-            if (b, c0) in own_bf:
-                return own_bf[b, c0][:]
-            tile = h1_bf if b == 1 else early_bf if c0 < HALF else late_bf
-            return tile[:, PACK * c0 : PACK * (c0 + width)]
+            return (h1_bf if b == 1 else line)[:, PACK * c0 : PACK * (c0 + width)]
 
-        def h_banks(first, width):
-            per = BANK // width
-            return [bank(first + u, [P, per, width]) for u in range(PACK // per)]
+        def h_banks(indices, width):
+            return [bank(index, [P, BANK // width, width]) for index in indices]
 
-        def h_pass(banks, b, c0, width, a):
-            per = BANK // width
-            codes, scales = w1_q[a, b]
-            for t in range(PACK):
+        def h_pass(banks, b, c0, a, tiles=range(PACK)):
+            per, width = banks[0].shape[1:]
+            codes, scales, first = w1_q[a, b]
+            for t in tiles:
+                cols = slice(first + P * t, first + P * (t + 1))
                 nc.tensor.matmul_mx(
                     out=banks[t // per][:, t % per, :],
-                    lhsT=codes[:, P * t : P * (t + 1)].bitcast(FP8X4),
-                    lhsT_scale=scales[:, P * t : P * (t + 1)],
+                    lhsT=codes[:, cols].bitcast(FP8X4),
+                    lhsT_scale=scales[:, cols],
                     rhs=v1[a][:, c0 : c0 + width].bitcast(FP4X4),
                     rhs_scale=planes[a][:, 0, c0 : c0 + width],
                     start=(a == 0 and t % per == 0),
@@ -207,71 +222,73 @@ def tile_list_unfollow_forecast_features_kernel(
 
         th = {}
 
-        def h_tanh(banks, b, c0, dst=None):
-            shape = [P, len(banks), banks[0].shape[2], banks[0].shape[1]]
-            th[b, c0] = sb("th%d_%d" % (b, c0), shape, F32)[:] if dst is None else dst
+        def h_tanh(banks, b, c0):
+            per, width = banks[0].shape[1:]
+            th[b, c0] = sb("th%d_%d" % (b, c0), [P, len(banks), width, per], F32)
             for u in range(len(banks)):
                 nc.scalar.activation(th[b, c0][:, u], banks[u][:].rearrange("p e n -> p n e"), ACT.Tanh)
 
-        def h_sums(first, b, c0, width):
-            banks = h_banks(first, width)
-            for a in range(passes):
-                h_pass(banks, b, c0, width, a)
-            return banks
-
-        def h_first(first, b, c0, width):
-            h_tanh(h_sums(first, b, c0, width), b, c0)
-
-        def h_gain(b, c0, width):
+        def h_first(indices, b, c0, width):
+            banks = h_banks(indices, width)
             per = BANK // width
+            for u in range(len(banks)):
+                for a in range(passes):
+                    h_pass(banks, b, c0, a, range(per * u, per * (u + 1)))
+            h_tanh(banks, b, c0)
+
+        def h_gain(b, c0):
+            regions, width, per = th[b, c0].shape[1:]
+            entries = RUN // PACK
             nc.vector.tensor_tensor(
-                h_bf(b, c0, width).rearrange("p (n u e) -> p n u e", u=PACK // per, e=per),
-                th[b, c0].rearrange("p u n e -> p n u e"),
-                g1[:, b : b + 1, :].rearrange("p n (u e) -> p n u e", e=per).to_broadcast([P, width, PACK // per, per]),
+                h_bf(b, c0, width).rearrange("p (c i u e) -> p c i u e", i=entries, u=regions, e=per),
+                th[b, c0][:].rearrange("p u (c i) e -> p c i u e", i=entries),
+                gains[:, RUN * b : RUN * (b + 1)]
+                .rearrange("p (c i u e) -> p c i u e", c=1, u=regions, e=per)
+                .to_broadcast([P, width // entries, entries, regions, per]),
                 MULT,
             )
 
         h_q = {}
 
-        def h_quantize(b, c0, width, tag):
+        def h_quantize(b, c0, width, tag=None):
             codes, scales = quantize("hq%d_%d" % (b, c0), h_bf(b, c0, width), tag)
             for c in range(c0, c0 + width, P):
                 h_q[b, c] = (codes, scales, c - c0)
 
         d_q = {}
 
-        def d_pass(banks, f, t, a):
-            nc.tensor.matmul_mx(
-                out=banks[t][:],
-                lhsT=w2c[:, a, P * t : P * (t + 1)].bitcast(FP8X4),
-                lhsT_scale=w2s[:, a, P * t : P * (t + 1)],
-                rhs=v2[a, f][:].bitcast(FP4X4),
-                rhs_scale=planes[a][:, 1, HALF * f : HALF * (f + 1)],
-                start=(a == 0),
-                stop=(a == passes - 1),
-            )
-
-        def d_sigmoid(banks, sig):
+        def d_first(f):
+            banks = [bank(1 + t, [P, HALF]) for t in range(PACK)]
+            sig = sb("sig%d" % f, [P, PACK, HALF], F32)
             for t in range(PACK):
+                for a in range(passes):
+                    nc.tensor.matmul_mx(
+                        out=banks[t][:],
+                        lhsT=w2c[:, a, P * t : P * (t + 1)].bitcast(FP8X4),
+                        lhsT_scale=w2s[:, a, P * t : P * (t + 1)],
+                        rhs=v2[a, f][:].bitcast(FP4X4),
+                        rhs_scale=planes[a][:, 1, HALF * f : HALF * (f + 1)],
+                        start=(a == 0),
+                        stop=(a == passes - 1),
+                    )
                 nc.scalar.activation(sig[:, t, :], banks[t][:], ACT.Sigmoid, bias=b2[:, t : t + 1])
+            return sig
 
         def d_gain(dst, sig):
             nc.vector.tensor_tensor(
                 dst.rearrange("p (c i t) -> p c t i", i=PACK, t=PACK),
                 sig.rearrange("p t (c i) -> p c t i", i=PACK),
-                g2[:].rearrange("p (c t i) -> p c t i", c=1, i=1).to_broadcast([P, HALF // PACK, PACK, PACK]),
+                gains[:, blocks * RUN : blocks * RUN + PACK * PACK]
+                .rearrange("p (c t i) -> p c t i", c=1, i=PACK)
+                .to_broadcast([P, sig.shape[2] // PACK, PACK, PACK]),
                 MULT,
             )
 
         out_v = out.rearrange("(i p) j -> p i j", p=P)
 
-        def y_banks(indices, width):
-            return [bank(index, [P, N // P // len(indices), width]) for index in indices]
-
         def y_passes(banks, c0, source, start=False, stop=False):
             per, width = banks[0].shape[1:]
-            codes, scales, at = d_q[c0 // HALF] if source == "d" else h_q[source, c0]
-            at = at + c0 % HALF if source == "d" else at
+            codes, scales, first = d_q[c0] if source == "d" else h_q[source, c0]
             for i in range(N // P):
                 rows = slice(P * i, P * (i + 1))
                 if source == "d":
@@ -282,100 +299,98 @@ def tile_list_unfollow_forecast_features_kernel(
                     out=banks[i // per][:, i % per, :],
                     lhsT=weights,
                     lhsT_scale=weight_scales,
-                    rhs=codes[:, at : at + width].bitcast(FP8X4),
-                    rhs_scale=scales[:, at : at + width],
+                    rhs=codes[:, first : first + width].bitcast(FP8X4),
+                    rhs_scale=scales[:, first : first + width],
                     start=(start and i % per == 0),
                     stop=(stop and i % per == per - 1),
                 )
 
         def y_open(indices, c0, width):
-            banks = y_banks(indices, width)
-            y_passes(banks, c0, "d", start=True)
+            banks = [bank(index, [P, N // P // len(indices), width]) for index in indices]
+            y_passes(banks, c0, 0, start=True)
             return banks
 
-        def y_close(banks, c0, source):
-            y_passes(banks, c0, source, stop=True)
+        def y_close(banks, c0):
+            y_passes(banks, c0, 1, stop=True)
             per, width = banks[0].shape[1:]
             for u in range(len(banks)):
                 res = sb("res%d_%d" % (c0, u), [P, per, width], F32)
                 nc.scalar.activation(res[:], banks[u][:], ACT.Gelu_apprx_tanh)
                 nc.sync.dma_start(out_v[:, per * u : per * (u + 1), c0 : c0 + width], res[:])
 
-        early = [h_banks(2 * c, CH) for c in range(4)]
+        early = [h_banks((2 * c, 2 * c + 1), CH) for c in range(3)]
         for a in range(passes):
-            for c in range(4):
-                h_pass(early[c], 0, CH * c, CH, a)
-        for c in range(4):
+            for c in range(3):
+                h_pass(early[c], 0, CH * c, a)
+        for c in range(3):
             h_tanh(early[c], 0, CH * c)
-        h_gain(0, 0, CH)
-        h_gain(0, CH, CH)
-        h_gain(0, HALF, CH)
+        h_first((6, 0), 0, 3 * CH, CH)
+        sig = [d_first(f) for f in range(halves)]
+        for c in range(4):
+            h_gain(0, CH * c)
+        d_gain(line[:, PACK * S : PACK * (S + CH)], sig[0][:, :, 0:CH])
 
-        def d_sums(first, f):
-            banks = [bank(first + t, [P, HALF]) for t in range(PACK)]
-            for t in range(PACK):
-                for a in range(passes):
-                    d_pass(banks, f, t, a)
-            return banks
-
-        d_banks = [d_sums(PACK * f, f) for f in range(halves)]
-        cast_w1(0, 1)
-        quantize_w1(0, 1)
-        h_quantize(0, 0, HALF, "raw01")
-        w4d_bf = sb("w4d_bf", [P, PACK * (N + HALF)], BF16)
-        nc.vector.tensor_copy(
-            w4d_bf[:, 0 : PACK * N].rearrange("p (c i t) -> p c t i", i=PACK, t=PACK),
-            w4_raw[:].rearrange("p t (c i) -> p c t i", i=PACK),
+        late_w1 = at("late_w1", [P, passes * PACK * KP], BF16, window_bytes // 2)
+        for a in range(passes):
+            nc.gpsimd.tensor_scalar(
+                late_w1[:, PACK * KP * a : PACK * KP * (a + 1)].rearrange("p (t m j) -> p m t j", t=PACK, j=PACK),
+                w1_raw[a, 1].rearrange("p j (m t) -> p m t j", t=PACK),
+                1.0,
+                0.0,
+                MULT,
+                ADD,
+            )
+        late_q = quantize("late_q", late_w1[:], "v2_11")
+        for a in range(passes):
+            w1_q[a, 1] = late_q + (KP * a,)
+        h_quantize(0, 0, S, "picked")
+        d_gain(line[:, PACK * (S + CH) : PACK * (S + HALF)], sig[0][:, :, CH:HALF])
+        d2_bf = sb("d2_bf", [P, PACK * CH], BF16)
+        d_gain(d2_bf[:], sig[1][:, :, 0:CH])
+        nc.gpsimd.tensor_scalar(
+            line[:, PACK * HALF : PACK * S].rearrange("p (c t) -> p c t", t=PACK),
+            w4_raw[:].rearrange("p t c -> p c t"),
+            1.0,
+            0.0,
+            MULT,
+            ADD,
         )
-        h_quantize(0, HALF, CH, None)
-        sig0 = sb("sig0", [P, PACK, HALF], F32)
-        d_sigmoid(d_banks[0], sig0[:])
-        d_gain(w4d_bf[:, PACK * N : PACK * (N + HALF)], sig0[:])
-        ahead = [h_banks(2 * c, CH) for c in range(2)]
-        for c in range(2):
-            h_pass(ahead[c], 1, CH * c, CH, 0)
-        cast_w1(1, 1, "th0_%d" % HALF)
-        quantize_w1(1, 1)
-        w4d_scales = placed.tile([P, N + HALF], U8, name="w4d_scales", align_bytes=64, offset=0)
-        d_q[0] = quantize("w4d", w4d_bf[:], None, w4d_scales) + (N,)
-        sig1 = placed.tile([P, PACK, HALF], F32, name="sig1", align_bytes=64, offset=N + HALF)
-        d_sigmoid(d_banks[1], sig1[:])
-        d_gain(late_bf[:, 0 : PACK * HALF], sig1[:])
 
-        last = S - CH
-        for c in range(2):
-            h_pass(ahead[c], 1, CH * c, CH, 1)
-            h_tanh(ahead[c], 1, CH * c)
-        h_first(4, 1, HALF, CH)
-        first = y_open((0, 1), 0, CH)
-        y_passes(first, 0, 0)
-        for c in range(2):
-            h_first(6 + c, 1, last + P * c, P)
+        h_first((5, 6), 1, 0, CH)
+        h_first((0, 1), 1, CH, CH)
+        late = [HALF + P * c for c in range(4)]
+        for c in range(4):
+            h_first((2 + c,), 1, late[c], P)
 
-        h_gain(1, 0, CH)
-        h_gain(1, CH, CH)
-        h_quantize(1, 0, CH, None)
-        d_q[1] = quantize("dq", late_bf[:, 0 : PACK * HALF]) + (0,)
-        h_gain(1, HALF, CH)
-        h_quantize(1, CH, CH, None)
-        own_bf[0, last] = sb("h0_last", [P, PACK * CH], BF16, "th1_%d" % CH)
-        h_gain(0, last, CH)
-        h_quantize(1, HALF, CH, None)
-        h_gain(1, last, P)
-        h_quantize(0, last, CH, None)
-        h_quantize(1, last, P, None)
-        h_gain(1, last + P, P)
-        h_quantize(1, last + P, P, None)
+        h_gain(1, 0)
+        h_gain(1, CH)
+        d_q[0] = quantize("w4d", line[:, PACK * HALF : PACK * (S + HALF)], "th1_0") + (N,)
+        h_quantize(1, 0, HALF)
+        d3_bf = line[:, PACK * S : PACK * (S + CH)]
+        d_gain(d3_bf, sig[1][:, :, CH:HALF])
 
-        second = y_open((2, 3), CH, CH)
-        y_passes(second, CH, 0)
-        y_close(first, 0, 1)
-        third = y_open((4, 5), HALF, CH)
-        y_close(second, CH, 1)
-        y_passes(third, HALF, 0)
-        fourth = y_open((6,), last, P)
-        y_close(third, HALF, 1)
-        fifth = y_open((7, 0, 1, 2), last + P, P)
-        for banks, c0 in ((fourth, last), (fifth, last + P)):
-            y_passes(banks, c0, 0)
-            y_close(banks, c0, 1)
+        def d_quantize(name, values, parts):
+            codes, scales = quantize(name, values)
+            for c in parts:
+                d_q[late[c]] = (codes, scales, late[c] % CH)
+
+        h_gain(1, late[0])
+        d_quantize("dq2", d2_bf[:], (0, 1))
+        h_gain(1, late[1])
+        h_quantize(1, late[0], P)
+        d_quantize("dq3", d3_bf, (2, 3))
+        h_gain(1, late[2])
+        h_quantize(1, late[1], P)
+        h_quantize(1, late[2], P)
+        h_gain(1, late[3])
+        h_quantize(1, late[3], P)
+
+        first = y_open((6, 0, 1, 2), 0, HALF)
+        y_passes(first, 0, "d")
+        parts = [y_open((3 + c,), late[c], P) for c in range(3)]
+        y_close(first, 0)
+        parts.append(y_open((6, 0), late[3], P))
+        for c in range(4):
+            y_passes(parts[c], late[c], "d")
+        for c in range(4):
+            y_close(parts[c], late[c])

@@ -55,6 +55,7 @@ def tile_list_unfollow_forecast_features_kernel(
             return psum.tile(shape, F32, name="bank%d" % index)
 
         window_bytes = 2 * T
+        third_piece = passes * window_bytes
 
         list1 = keep.tile([P, S // 16], U16, name="list1")
         list2 = keep.tile([P, S // 16], U16, name="list2")
@@ -99,7 +100,10 @@ def tile_list_unfollow_forecast_features_kernel(
         w1_raw = {}
 
         def load_w1(a, b):
-            raw = sb("raw%d%d" % (a, b), [P, PACK, KP], F32)[:]
+            if (a, b) == (0, 1):
+                raw = at("raw01", [P, PACK, KP], F32, third_piece)[:]
+            else:
+                raw = sb("raw%d%d" % (a, b), [P, PACK, KP], F32)[:]
             nc.sync.dma_start(raw, w1[KP * a : KP * (a + 1), KP * b : KP * (b + 1)].rearrange("(p j) c -> p j c", j=PACK))
             w1_raw[a, b] = raw
 
@@ -110,10 +114,10 @@ def tile_list_unfollow_forecast_features_kernel(
                     planes[a][QUAD * q : QUAD * q + SROWS].bitcast(I32), picked[row : row + SROWS].bitcast(I32)
                 )
 
-        def quantize(name, values, tag=None):
+        def quantize(name, values, tag=None, place=None):
             width = values.shape[1] // PACK
             codes = sb(name + "c", [P, width], U32)
-            scales = sb(name + "s", [P, width], U8, tag)
+            scales = sb(name + "s", [P, width], U8, tag) if place is None else at(name + "s", [P, width], U8, place)
             nc.vector.quantize_mx(out=codes[:].bitcast(FP8X4), scales=scales[:], in_=values)
             return codes, scales
 
@@ -250,15 +254,15 @@ def tile_list_unfollow_forecast_features_kernel(
 
         h_q = {}
 
-        def h_quantize(b, c0, width, tag=None):
-            codes, scales = quantize("hq%d_%d" % (b, c0), h_bf(b, c0, width), tag)
+        def h_quantize(b, c0, width, place=None):
+            codes, scales = quantize("hq%d_%d" % (b, c0), h_bf(b, c0, width), None, place)
             for c in range(c0, c0 + width, P):
                 h_q[b, c] = (codes, scales, c - c0)
 
         d_q = {}
 
-        def d_first(f):
-            banks = [bank(1 + t, [P, HALF]) for t in range(PACK)]
+        def d_first(f, indices):
+            banks = [bank(index, [P, HALF]) for index in indices]
             sig = sb("sig%d" % f, [P, PACK, HALF], F32)
             for t in range(PACK):
                 for a in range(passes):
@@ -286,10 +290,10 @@ def tile_list_unfollow_forecast_features_kernel(
 
         out_v = out.rearrange("(i p) j -> p i j", p=P)
 
-        def y_passes(banks, c0, source, start=False, stop=False):
+        def y_passes(banks, c0, source, start=False, stop=False, tiles=range(N // P)):
             per, width = banks[0].shape[1:]
             codes, scales, first = d_q[c0] if source == "d" else h_q[source, c0]
-            for i in range(N // P):
+            for i in tiles:
                 rows = slice(P * i, P * (i + 1))
                 if source == "d":
                     weights, weight_scales = d_q[0][0][:, rows].bitcast(FP8X4), d_q[0][1][:, rows]
@@ -310,10 +314,11 @@ def tile_list_unfollow_forecast_features_kernel(
             y_passes(banks, c0, 0, start=True)
             return banks
 
-        def y_close(banks, c0):
-            y_passes(banks, c0, 1, stop=True)
+        def y_close(banks, c0, sources):
             per, width = banks[0].shape[1:]
             for u in range(len(banks)):
+                for source in sources:
+                    y_passes(banks, c0, source, stop=(source == 1), tiles=range(per * u, per * (u + 1)))
                 res = sb("res%d_%d" % (c0, u), [P, per, width], F32)
                 nc.scalar.activation(res[:], banks[u][:], ACT.Gelu_apprx_tanh)
                 nc.sync.dma_start(out_v[:, per * u : per * (u + 1), c0 : c0 + width], res[:])
@@ -325,28 +330,27 @@ def tile_list_unfollow_forecast_features_kernel(
         for c in range(3):
             h_tanh(early[c], 0, CH * c)
         h_first((6, 0), 0, 3 * CH, CH)
-        sig = [d_first(f) for f in range(halves)]
+        third_bf = sb("third_bf", [P, PACK * KP], BF16)
+        nc.scalar.copy(dealt(third_bf[:]), rows_of(0, 1))
+        sig = [d_first(0, (1, 2, 3, 4)), d_first(1, (5, 6, 0, 1))]
         for c in range(4):
             h_gain(0, CH * c)
-        d_gain(line[:, PACK * S : PACK * (S + CH)], sig[0][:, :, 0:CH])
 
-        late_w1 = at("late_w1", [P, passes * PACK * KP], BF16, window_bytes // 2)
-        for a in range(passes):
-            nc.gpsimd.tensor_scalar(
-                late_w1[:, PACK * KP * a : PACK * KP * (a + 1)].rearrange("p (t m j) -> p m t j", t=PACK, j=PACK),
-                w1_raw[a, 1].rearrange("p j (m t) -> p m t j", t=PACK),
-                1.0,
-                0.0,
-                MULT,
-                ADD,
-            )
-        late_q = quantize("late_q", late_w1[:], "v2_11")
-        for a in range(passes):
-            w1_q[a, 1] = late_q + (KP * a,)
-        h_quantize(0, 0, S, "picked")
-        d_gain(line[:, PACK * (S + CH) : PACK * (S + HALF)], sig[0][:, :, CH:HALF])
-        d2_bf = sb("d2_bf", [P, PACK * CH], BF16)
-        d_gain(d2_bf[:], sig[1][:, :, 0:CH])
+        last_bf = at("last_bf", [P, PACK * KP], BF16, window_bytes - PACK * KP)
+        nc.gpsimd.tensor_scalar(
+            last_bf[:].rearrange("p (t m j) -> p m t j", t=PACK, j=PACK),
+            w1_raw[1, 1].rearrange("p j (m t) -> p m t j", t=PACK),
+            1.0,
+            0.0,
+            MULT,
+            ADD,
+        )
+        w1_q[1, 1] = quantize("w1q11", last_bf[:], None, third_piece) + (0,)
+        w1_q[0, 1] = quantize("w1q01", third_bf[:]) + (0,)
+        h_quantize(0, 0, S, third_piece + KP)
+        d_gain(line[:, PACK * S : PACK * (S + HALF)], sig[0][:])
+        d1_bf = sb("d1_bf", [P, PACK * HALF], BF16)
+        d_gain(d1_bf[:], sig[1][:])
         nc.gpsimd.tensor_scalar(
             line[:, PACK * HALF : PACK * S].rearrange("p (c t) -> p c t", t=PACK),
             w4_raw[:].rearrange("p t c -> p c t"),
@@ -356,41 +360,40 @@ def tile_list_unfollow_forecast_features_kernel(
             ADD,
         )
 
-        h_first((5, 6), 1, 0, CH)
-        h_first((0, 1), 1, CH, CH)
+        h_first((2, 3), 1, 0, CH)
+        h_first((4, 5), 1, CH, CH)
         late = [HALF + P * c for c in range(4)]
         for c in range(4):
-            h_first((2 + c,), 1, late[c], P)
+            h_first(((6 + c) % GAIN_BANK,), 1, late[c], P)
 
         h_gain(1, 0)
+        d_q[0] = quantize("w4d", line[:, PACK * HALF : PACK * (S + HALF)]) + (N,)
+        d_q[CH] = d_q[0][0:2] + (N + CH,)
+        h_quantize(1, 0, CH)
         h_gain(1, CH)
-        d_q[0] = quantize("w4d", line[:, PACK * HALF : PACK * (S + HALF)], "th1_0") + (N,)
-        h_quantize(1, 0, HALF)
-        d3_bf = line[:, PACK * S : PACK * (S + CH)]
-        d_gain(d3_bf, sig[1][:, :, CH:HALF])
-
-        def d_quantize(name, values, parts):
-            codes, scales = quantize(name, values)
-            for c in parts:
-                d_q[late[c]] = (codes, scales, late[c] % CH)
-
+        late_d = quantize("late_d", d1_bf[:])
+        for c in late:
+            d_q[c] = late_d + (c - HALF,)
+        h_quantize(1, CH, CH)
         h_gain(1, late[0])
-        d_quantize("dq2", d2_bf[:], (0, 1))
         h_gain(1, late[1])
         h_quantize(1, late[0], P)
-        d_quantize("dq3", d3_bf, (2, 3))
         h_gain(1, late[2])
         h_quantize(1, late[1], P)
         h_quantize(1, late[2], P)
         h_gain(1, late[3])
         h_quantize(1, late[3], P)
 
-        first = y_open((6, 0, 1, 2), 0, HALF)
+        first = y_open((3, 4), 0, CH)
+        second = y_open((5, 6), CH, CH)
         y_passes(first, 0, "d")
-        parts = [y_open((3 + c,), late[c], P) for c in range(3)]
-        y_close(first, 0)
-        parts.append(y_open((6, 0), late[3], P))
+        y_passes(second, CH, "d")
+        parts = [y_open((c,), late[c], P) for c in range(3)]
+        y_close(first, 0, (1,))
+        y_close(second, CH, (1,))
+        parts.append(y_open((3, 4), late[3], P))
+        y_passes(parts[0], late[0], "d")
         for c in range(4):
-            y_passes(parts[c], late[c], "d")
-        for c in range(4):
-            y_close(parts[c], late[c])
+            if c + 1 < 4:
+                y_passes(parts[c + 1], late[c + 1], "d")
+            y_close(parts[c], late[c], (1,))

@@ -29,6 +29,8 @@ CH = 256
 HALF = 512
 BANK = 512
 RUN = 32
+EIGHT = 8
+SHARE = 96
 GAIN_BANK = 7
 
 
@@ -64,13 +66,13 @@ def tile_list_unfollow_forecast_features_kernel(
         picked = sb("picked", [P, 2, S], U8)
         planes = [sb("plane%d" % a, [P, 2, S], U8) for a in range(passes)]
         g1 = sb("g1", [P, blocks, PACK], F32)
-        g2 = sb("g2", [P, PACK], F32)
+        rows = sb("rows", [P, P], F32)
         b2 = sb("b2", [P, PACK], F32)
         w2s_raw = sb("w2s_raw", [P, passes, G], U8)
         w3s = sb("w3s", [P, blocks, N], U8)
         w2_raw = sb("w2_raw", [P, passes, G], I32)
-        w2c = sb("w2c", [P, passes, G], U32)
-        w2s = sb("w2s", [P, passes, G], U8)
+        w2c = sb("w2c", [P, PACK, passes, P], U32)
+        w2s = sb("w2s", [P, PACK, passes, P], U8)
         w4_raw = sb("w4_raw", [P, PACK, N], F32)
         w3c = sb("w3c", [P, blocks, 2 * N], U8)
         ident = sb("ident", [P, P], F32)
@@ -90,8 +92,9 @@ def tile_list_unfollow_forecast_features_kernel(
                     scales[:, SROWS * q : SROWS * (q + 1), :].rearrange("a r c -> r a c").bitcast(I32),
                 )
 
-        nc.gpsimd.memset(w2s_raw[:].bitcast(I32), 0)
+        nc.gpsimd.memset(rows[:], 0.0)
         make_identity(nc, ident[:])
+        nc.gpsimd.memset(w2s_raw[:].bitcast(I32), 0)
         nc.gpsimd.memset(w3s[:].bitcast(I32), 0)
 
         def load_tab(a):
@@ -134,9 +137,12 @@ def tile_list_unfollow_forecast_features_kernel(
         nc.sync.dma_start(swin[LIVE:P].bitcast(I32), tab_scales.rearrange("a r c -> (a r) c").bitcast(I32))
         nc.sync.dma_start(list2[:], offs2)
         load_tab(0)
-        load_scale_rows(w2s_raw, w2_scales)
         nc.sync.dma_start(g1[:], gain1.rearrange("(b p t) -> p b t", b=blocks, t=PACK))
-        nc.sync.dma_start(g2[:], gain2.rearrange("(p t) -> p t", t=PACK))
+        for v, vector in enumerate((gain2, bias2)):
+            nc.sync.dma_start(
+                rows[PACK * v : PACK * (v + 1)].rearrange("t (b i) -> t b i", i=EIGHT),
+                vector.rearrange("(b t i) -> t b i", t=PACK, i=EIGHT),
+            )
         load_w1(0, 0)
         load_w1(1, 0)
 
@@ -144,15 +150,19 @@ def tile_list_unfollow_forecast_features_kernel(
         gather(picked[:, 1, :], swin, list2, 0, S)
         move_scales(0)
         load_tab(1)
+        load_scale_rows(w2s_raw, w2_scales)
         nc.sync.dma_start(w2_raw[:], w2_words.rearrange("a p c i -> p a (c i)").bitcast(I32))
         move_scales(1)
-        load_w1(0, 1)
-        nc.sync.dma_start(b2[:], bias2.rearrange("(p t) -> p t", t=PACK))
         load_w1(1, 1)
-        nc.sync.dma_start(w4_raw[:], w4.rearrange("(p j) n -> p j n", j=PACK))
+        load_w1(0, 1)
+        for t in range(PACK):
+            nc.sync.dma_start(w4_raw[:, t, :], w4.rearrange("(b t i) n -> t b i n", t=PACK, i=EIGHT)[t])
         nc.sync.dma_start(w3c[:].bitcast(I32), w3_words.rearrange("a p n -> p a n").bitcast(I32))
         load_scale_rows(w3s, w3_scales)
 
+        columns = bank(1, [P, P])
+        nc.tensor.transpose(columns[:], rows[:], ident[:])
+        nc.scalar.copy(b2[:], columns[:, PACK : 2 * PACK])
         spread = sb("spread", [P, P], F32)
         nc.scalar.copy(
             spread[:, 0 : blocks * RUN].rearrange("p (b i t) -> p b i t", b=blocks, t=PACK),
@@ -160,7 +170,7 @@ def tile_list_unfollow_forecast_features_kernel(
         )
         nc.scalar.copy(
             spread[:, blocks * RUN : P].rearrange("p (c t i) -> p c t i", t=PACK, i=PACK),
-            g2[:].rearrange("p (c t i) -> p c t i", c=1, i=1).to_broadcast([P, PACK, PACK, PACK]),
+            columns[:, 0:PACK].rearrange("p (c t i) -> p c t i", c=1, i=1).to_broadcast([P, PACK, PACK, PACK]),
         )
         turned_ps = bank(0, [P, P])
         nc.tensor.transpose(turned_ps[:], spread[:], ident[:])
@@ -170,11 +180,7 @@ def tile_list_unfollow_forecast_features_kernel(
         nc.tensor.transpose(gains[:], turned[:], ident[:])
 
         v1 = [sb("v1_%d" % a, [P, S], U16) for a in range(passes)]
-        v2 = {}
-
-        def gather_v2(a, f, tag=None):
-            v2[a, f] = sb("v2_%d%d" % (a, f), [P, HALF], U16, tag)
-            gather(v2[a, f][:], wwin[a], list2, HALF * f, HALF * (f + 1))
+        v2 = [sb("v2_0", [P, S], U16, "raw00"), sb("v2_1", [P, S], U16)]
 
         w1_q = {}
 
@@ -184,21 +190,20 @@ def tile_list_unfollow_forecast_features_kernel(
             w1_q[a, 0] = quantize("w1q%d" % a, grouped[:]) + (0,)
 
         gather(v1[0][:], wwin[0], list1, 0, S)
-        nc.vector.tensor_copy(
-            w2s[:].rearrange("p a (t m) -> p a m t", t=PACK), w2s_raw[:].rearrange("p a (m t) -> p a m t", t=PACK)
-        )
         early_w1(0)
-        gather_v2(0, 0, "raw00")
+        gather(v2[0][:], wwin[0], list2, 0, S)
         early_w1(1)
         nc.scalar.copy(
-            w2c[:].rearrange("p a (t m) -> p a m t", t=PACK),
-            w2_raw[:].bitcast(U32).rearrange("p a (m t) -> p a m t", t=PACK),
+            w2c[:].rearrange("p t a (b i) -> p t (a b) i", i=EIGHT),
+            w2_raw[:].bitcast(U32).rearrange("p a (b t i) -> p t (a b) i", t=PACK, i=EIGHT),
+        )
+        nc.scalar.copy(
+            w2s[:].bitcast(U32).rearrange("p t a (b i) -> p t (a b) i", i=2),
+            w2s_raw[:].bitcast(U32).rearrange("p a (b t i) -> p t (a b) i", t=PACK, i=2),
         )
         for f in range(halves):
             gather(v1[1][:, HALF * f : HALF * (f + 1)], wwin[1], list1, HALF * f, HALF * (f + 1))
-        for f in range(halves):
-            gather_v2(1, f)
-        gather_v2(0, 1, "picked")
+        gather(v2[1][:], wwin[1], list2, 0, S)
 
         line = sb("line", [P, PACK * (S + HALF)], BF16)
         h1_bf = sb("h1_bf", [P, PACK * S], BF16)
@@ -268,9 +273,9 @@ def tile_list_unfollow_forecast_features_kernel(
                 for a in range(passes):
                     nc.tensor.matmul_mx(
                         out=banks[t][:],
-                        lhsT=w2c[:, a, P * t : P * (t + 1)].bitcast(FP8X4),
-                        lhsT_scale=w2s[:, a, P * t : P * (t + 1)],
-                        rhs=v2[a, f][:].bitcast(FP4X4),
+                        lhsT=w2c[:, t, a, :].bitcast(FP8X4),
+                        lhsT_scale=w2s[:, t, a, :],
+                        rhs=v2[a][:, HALF * f : HALF * (f + 1)].bitcast(FP4X4),
                         rhs_scale=planes[a][:, 1, HALF * f : HALF * (f + 1)],
                         start=(a == 0),
                         stop=(a == passes - 1),
@@ -294,11 +299,11 @@ def tile_list_unfollow_forecast_features_kernel(
             per, width = banks[0].shape[1:]
             codes, scales, first = d_q[c0] if source == "d" else h_q[source, c0]
             for i in tiles:
-                rows = slice(P * i, P * (i + 1))
+                cols = slice(P * i, P * (i + 1))
                 if source == "d":
-                    weights, weight_scales = d_q[0][0][:, rows].bitcast(FP8X4), d_q[0][1][:, rows]
+                    weights, weight_scales = d_q[0][0][:, cols].bitcast(FP8X4), d_q[0][1][:, cols]
                 else:
-                    weights, weight_scales = w3c[:, source, 2 * P * i : 2 * P * (i + 1)].bitcast(FP4X4), w3s[:, source, rows]
+                    weights, weight_scales = w3c[:, source, 2 * P * i : 2 * P * (i + 1)].bitcast(FP4X4), w3s[:, source, cols]
                 nc.tensor.matmul_mx(
                     out=banks[i // per][:, i % per, :],
                     lhsT=weights,
@@ -331,7 +336,7 @@ def tile_list_unfollow_forecast_features_kernel(
             h_tanh(early[c], 0, CH * c)
         h_first((6, 0), 0, 3 * CH, CH)
         third_bf = sb("third_bf", [P, PACK * KP], BF16)
-        nc.scalar.copy(dealt(third_bf[:]), rows_of(0, 1))
+        nc.scalar.copy(dealt(third_bf[:])[:, 0:SHARE], rows_of(0, 1)[:, 0:SHARE])
         sig = [d_first(0, (1, 2, 3, 4)), d_first(1, (5, 6, 0, 1))]
         for c in range(4):
             h_gain(0, CH * c)
@@ -340,6 +345,14 @@ def tile_list_unfollow_forecast_features_kernel(
         nc.gpsimd.tensor_scalar(
             last_bf[:].rearrange("p (t m j) -> p m t j", t=PACK, j=PACK),
             w1_raw[1, 1].rearrange("p j (m t) -> p m t j", t=PACK),
+            1.0,
+            0.0,
+            MULT,
+            ADD,
+        )
+        nc.gpsimd.tensor_scalar(
+            third_bf[:].rearrange("p (t m j) -> p m t j", t=PACK, j=PACK)[:, SHARE:P],
+            w1_raw[0, 1].rearrange("p j (m t) -> p m t j", t=PACK)[:, SHARE:P],
             1.0,
             0.0,
             MULT,
@@ -371,25 +384,24 @@ def tile_list_unfollow_forecast_features_kernel(
         d_q[CH] = d_q[0][0:2] + (N + CH,)
         h_quantize(1, 0, CH)
         h_gain(1, CH)
-        late_d = quantize("late_d", d1_bf[:])
-        for c in late:
-            d_q[c] = late_d + (c - HALF,)
+
+        def d_quantize(c0):
+            d_q[c0] = quantize("dq%d" % c0, d1_bf[:, PACK * (c0 - HALF) : PACK * (c0 - HALF + P)]) + (0,)
+
+        d_quantize(late[0])
         h_quantize(1, CH, CH)
-        h_gain(1, late[0])
-        h_gain(1, late[1])
-        h_quantize(1, late[0], P)
-        h_gain(1, late[2])
-        h_quantize(1, late[1], P)
-        h_quantize(1, late[2], P)
-        h_gain(1, late[3])
-        h_quantize(1, late[3], P)
+        for c in range(4):
+            h_gain(1, late[c])
+            if c + 1 < 4:
+                d_quantize(late[c + 1])
+            h_quantize(1, late[c], P)
 
         first = y_open((3, 4), 0, CH)
         second = y_open((5, 6), CH, CH)
         y_passes(first, 0, "d")
-        y_passes(second, CH, "d")
         parts = [y_open((c,), late[c], P) for c in range(3)]
         y_close(first, 0, (1,))
+        y_passes(second, CH, "d")
         y_close(second, CH, (1,))
         parts.append(y_open((3, 4), late[3], P))
         y_passes(parts[0], late[0], "d")

@@ -363,7 +363,7 @@ def tile_list_unfollow_forecast_features_kernel(
         h_quantize(0, 0, S, third_piece + KP)
         d_gain(line[:, PACK * S : PACK * (S + HALF)], sig[0][:])
         d1_bf = sb("d1_bf", [P, PACK * HALF], BF16)
-        d_gain(d1_bf[:], sig[1][:])
+        d_gain(d1_bf[:, 0 : PACK * (HALF - P)], sig[1][:, :, 0 : HALF - P])
         nc.gpsimd.tensor_scalar(
             line[:, PACK * HALF : PACK * S].rearrange("p (c t) -> p c t", t=PACK),
             w4_raw[:].rearrange("p t c -> p c t"),
@@ -371,6 +371,15 @@ def tile_list_unfollow_forecast_features_kernel(
             0.0,
             MULT,
             ADD,
+        )
+
+        nc.gpsimd.tensor_tensor(
+            d1_bf[:, PACK * (HALF - P) : PACK * HALF].rearrange("p (n t) -> p n t", t=PACK),
+            sig[1][:, :, HALF - P : HALF].rearrange("p t n -> p n t"),
+            spread[:, blocks * RUN : blocks * RUN + PACK * PACK]
+            .rearrange("p (n t i) -> p i n t", n=1, i=PACK)[:, 0]
+            .to_broadcast([P, P, PACK]),
+            MULT,
         )
 
         h_first((2, 3), 1, 0, CH)

@@ -30,7 +30,6 @@ HALF = 512
 BANK = 512
 RUN = 32
 EIGHT = 8
-SHARE = 96
 GAIN_BANK = 7
 
 
@@ -58,6 +57,8 @@ def tile_list_unfollow_forecast_features_kernel(
 
         window_bytes = 2 * T
         third_piece = passes * window_bytes
+        first_sig = third_piece + 4 * KP
+        head_tanh = first_sig + 4 * PACK * HALF
 
         list1 = keep.tile([P, S // 16], U16, name="list1")
         list2 = keep.tile([P, S // 16], U16, name="list2")
@@ -206,9 +207,12 @@ def tile_list_unfollow_forecast_features_kernel(
         gather(v2[1][:], wwin[1], list2, 0, S)
 
         line = sb("line", [P, PACK * (S + HALF)], BF16)
+        own_bf = {(1, 0): sb("head_bf", [P, PACK * CH], BF16)}
         h1_bf = sb("h1_bf", [P, PACK * S], BF16)
 
         def h_bf(b, c0, width):
+            if (b, c0) in own_bf:
+                return own_bf[b, c0][:]
             return (h1_bf if b == 1 else line)[:, PACK * c0 : PACK * (c0 + width)]
 
         def h_banks(indices, width):
@@ -233,7 +237,10 @@ def tile_list_unfollow_forecast_features_kernel(
 
         def h_tanh(banks, b, c0):
             per, width = banks[0].shape[1:]
-            th[b, c0] = sb("th%d_%d" % (b, c0), [P, len(banks), width, per], F32)
+            if (b, c0) == (1, 0):
+                th[b, c0] = at("th_head", [P, len(banks), width, per], F32, head_tanh)
+            else:
+                th[b, c0] = sb("th%d_%d" % (b, c0), [P, len(banks), width, per], F32)
             for u in range(len(banks)):
                 nc.scalar.activation(th[b, c0][:, u], banks[u][:].rearrange("p e n -> p n e"), ACT.Tanh)
 
@@ -268,7 +275,10 @@ def tile_list_unfollow_forecast_features_kernel(
 
         def d_first(f, indices):
             banks = [bank(index, [P, HALF]) for index in indices]
-            sig = sb("sig%d" % f, [P, PACK, HALF], F32)
+            if f == 0:
+                sig = at("sig0", [P, PACK, HALF], F32, first_sig)
+            else:
+                sig = sb("sig1", [P, PACK, HALF], F32)
             for t in range(PACK):
                 for a in range(passes):
                     nc.tensor.matmul_mx(
@@ -336,7 +346,7 @@ def tile_list_unfollow_forecast_features_kernel(
             h_tanh(early[c], 0, CH * c)
         h_first((6, 0), 0, 3 * CH, CH)
         third_bf = sb("third_bf", [P, PACK * KP], BF16)
-        nc.scalar.copy(dealt(third_bf[:])[:, 0:SHARE], rows_of(0, 1)[:, 0:SHARE])
+        nc.scalar.copy(dealt(third_bf[:]), rows_of(0, 1))
         sig = [d_first(0, (1, 2, 3, 4)), d_first(1, (5, 6, 0, 1))]
         for c in range(4):
             h_gain(0, CH * c)
@@ -350,20 +360,12 @@ def tile_list_unfollow_forecast_features_kernel(
             MULT,
             ADD,
         )
-        nc.gpsimd.tensor_scalar(
-            third_bf[:].rearrange("p (t m j) -> p m t j", t=PACK, j=PACK)[:, SHARE:P],
-            w1_raw[0, 1].rearrange("p j (m t) -> p m t j", t=PACK)[:, SHARE:P],
-            1.0,
-            0.0,
-            MULT,
-            ADD,
-        )
         w1_q[1, 1] = quantize("w1q11", last_bf[:], None, third_piece) + (0,)
         w1_q[0, 1] = quantize("w1q01", third_bf[:]) + (0,)
         h_quantize(0, 0, S, third_piece + KP)
         d_gain(line[:, PACK * S : PACK * (S + HALF)], sig[0][:])
-        d1_bf = sb("d1_bf", [P, PACK * HALF], BF16)
-        d_gain(d1_bf[:, 0 : PACK * (HALF - P)], sig[1][:, :, 0 : HALF - P])
+        d1_bf = sb("d1_bf", [P, PACK * CH], BF16)
+        d_gain(d1_bf[:, 0 : PACK * CH], sig[1][:, :, 0:CH])
         nc.gpsimd.tensor_scalar(
             line[:, PACK * HALF : PACK * S].rearrange("p (c t) -> p c t", t=PACK),
             w4_raw[:].rearrange("p t c -> p c t"),
@@ -371,15 +373,6 @@ def tile_list_unfollow_forecast_features_kernel(
             0.0,
             MULT,
             ADD,
-        )
-
-        nc.gpsimd.tensor_tensor(
-            d1_bf[:, PACK * (HALF - P) : PACK * HALF].rearrange("p (n t) -> p n t", t=PACK),
-            sig[1][:, :, HALF - P : HALF].rearrange("p t n -> p n t"),
-            spread[:, blocks * RUN : blocks * RUN + PACK * PACK]
-            .rearrange("p (n t i) -> p i n t", n=1, i=PACK)[:, 0]
-            .to_broadcast([P, P, PACK]),
-            MULT,
         )
 
         h_first((2, 3), 1, 0, CH)
@@ -393,26 +386,39 @@ def tile_list_unfollow_forecast_features_kernel(
         d_q[CH] = d_q[0][0:2] + (N + CH,)
         h_quantize(1, 0, CH)
         h_gain(1, CH)
+        d_gain(line[:, PACK * S : PACK * (S + P)], sig[1][:, :, CH : CH + P])
+        end_bf = sb("end_bf", [P, PACK * P], BF16, "head_bf")
+        nc.gpsimd.tensor_tensor(
+            end_bf[:].rearrange("p (n t) -> p n t", t=PACK),
+            sig[1][:, :, HALF - P : HALF].rearrange("p t n -> p n t"),
+            spread[:, blocks * RUN : blocks * RUN + PACK * PACK]
+            .rearrange("p (n t i) -> p i n t", n=1, i=PACK)[:, 0]
+            .to_broadcast([P, P, PACK]),
+            MULT,
+        )
+        late_d = [d1_bf[:, 0 : PACK * P], d1_bf[:, PACK * P : PACK * CH], line[:, PACK * S : PACK * (S + P)], end_bf[:]]
 
         def d_quantize(c0):
-            d_q[c0] = quantize("dq%d" % c0, d1_bf[:, PACK * (c0 - HALF) : PACK * (c0 - HALF + P)]) + (0,)
+            d_q[c0] = quantize("dq%d" % c0, late_d[late.index(c0)], None, head_tanh + c0 - HALF) + (0,)
 
         d_quantize(late[0])
         h_quantize(1, CH, CH)
-        for c in range(4):
+        for c in range(3):
             h_gain(1, late[c])
-            if c + 1 < 4:
-                d_quantize(late[c + 1])
+            d_quantize(late[c + 1])
             h_quantize(1, late[c], P)
+        own_bf[1, late[3]] = sb("tail_bf", [P, PACK * P], BF16, "head_bf")
+        h_gain(1, late[3])
+        h_quantize(1, late[3], P)
 
-        first = y_open((3, 4), 0, CH)
-        second = y_open((5, 6), CH, CH)
+        first = y_open((1, 2), 0, CH)
+        second = y_open((3, 4), CH, CH)
         y_passes(first, 0, "d")
-        parts = [y_open((c,), late[c], P) for c in range(3)]
+        parts = [y_open(((5, 6, 0)[c],), late[c], P) for c in range(3)]
         y_close(first, 0, (1,))
         y_passes(second, CH, "d")
         y_close(second, CH, (1,))
-        parts.append(y_open((3, 4), late[3], P))
+        parts.append(y_open((1, 2), late[3], P))
         y_passes(parts[0], late[0], "d")
         for c in range(4):
             if c + 1 < 4:

@@ -68,7 +68,7 @@ def tile_list_unfollow_forecast_features_kernel(
         planes = [sb("plane%d" % a, [P, 2, S], U8) for a in range(passes)]
         g1 = sb("g1", [P, blocks, PACK], F32)
         rows = sb("rows", [P, P], F32)
-        b2 = sb("b2", [P, PACK], F32)
+        gain_bias = sb("gain_bias", [P, 2, PACK], F32)
         w2s_raw = sb("w2s_raw", [P, passes, G], U8)
         w3s = sb("w3s", [P, blocks, N], U8)
         w2_raw = sb("w2_raw", [P, passes, G], I32)
@@ -163,7 +163,7 @@ def tile_list_unfollow_forecast_features_kernel(
 
         columns = bank(1, [P, P])
         nc.tensor.transpose(columns[:], rows[:], ident[:])
-        nc.scalar.copy(b2[:], columns[:, PACK : 2 * PACK])
+        nc.scalar.copy(gain_bias[:], columns[:, 0 : 2 * PACK].rearrange("p (v t) -> p v t", t=PACK))
         spread = sb("spread", [P, P], F32)
         nc.scalar.copy(
             spread[:, 0 : blocks * RUN].rearrange("p (b i t) -> p b i t", b=blocks, t=PACK),
@@ -207,12 +207,12 @@ def tile_list_unfollow_forecast_features_kernel(
         gather(v2[1][:], wwin[1], list2, 0, S)
 
         line = sb("line", [P, PACK * (S + HALF)], BF16)
-        own_bf = {(1, 0): sb("head_bf", [P, PACK * CH], BF16)}
+        own_bf = {(1, 0): sb("head_bf", [P, PACK * CH], BF16)[:]}
         h1_bf = sb("h1_bf", [P, PACK * S], BF16)
 
         def h_bf(b, c0, width):
             if (b, c0) in own_bf:
-                return own_bf[b, c0][:]
+                return own_bf[b, c0]
             return (h1_bf if b == 1 else line)[:, PACK * c0 : PACK * (c0 + width)]
 
         def h_banks(indices, width):
@@ -290,7 +290,7 @@ def tile_list_unfollow_forecast_features_kernel(
                         start=(a == 0),
                         stop=(a == passes - 1),
                     )
-                nc.scalar.activation(sig[:, t, :], banks[t][:], ACT.Sigmoid, bias=b2[:, t : t + 1])
+                nc.scalar.activation(sig[:, t, :], banks[t][:], ACT.Sigmoid, bias=gain_bias[:, 1, t : t + 1])
             return sig
 
         def d_gain(dst, sig):
@@ -386,28 +386,28 @@ def tile_list_unfollow_forecast_features_kernel(
         d_q[CH] = d_q[0][0:2] + (N + CH,)
         h_quantize(1, 0, CH)
         h_gain(1, CH)
-        d_gain(line[:, PACK * S : PACK * (S + P)], sig[1][:, :, CH : CH + P])
-        end_bf = sb("end_bf", [P, PACK * P], BF16, "head_bf")
+        d_gain(line[:, PACK * S : PACK * (S + CH)], sig[1][:, :, CH:HALF])
+        own_bf[1, late[0]] = sb("side_bf", [P, PACK * P], BF16, "head_bf")[:]
         nc.gpsimd.tensor_tensor(
-            end_bf[:].rearrange("p (n t) -> p n t", t=PACK),
-            sig[1][:, :, HALF - P : HALF].rearrange("p t n -> p n t"),
-            spread[:, blocks * RUN : blocks * RUN + PACK * PACK]
-            .rearrange("p (n t i) -> p i n t", n=1, i=PACK)[:, 0]
-            .to_broadcast([P, P, PACK]),
+            own_bf[1, late[0]].rearrange("p (n t) -> p n t", t=PACK),
+            th[1, late[0]][:, 0],
+            g1[:, 1:2, :].to_broadcast([P, P, PACK]),
             MULT,
         )
-        late_d = [d1_bf[:, 0 : PACK * P], d1_bf[:, PACK * P : PACK * CH], line[:, PACK * S : PACK * (S + P)], end_bf[:]]
+        late_d = [(d1_bf if c < 2 else line[:, PACK * S :])[:, PACK * P * (c % 2) : PACK * P * (c % 2 + 1)] for c in range(4)]
 
-        def d_quantize(c0):
-            d_q[c0] = quantize("dq%d" % c0, late_d[late.index(c0)], None, head_tanh + c0 - HALF) + (0,)
+        def d_quantize(c):
+            d_q[late[c]] = quantize("dq%d" % c, late_d[c], None, head_tanh + P * c) + (0,)
 
-        d_quantize(late[0])
+        d_quantize(0)
         h_quantize(1, CH, CH)
-        for c in range(3):
+        h_quantize(1, late[0], P)
+        d_quantize(1)
+        for c in range(1, 3):
             h_gain(1, late[c])
-            d_quantize(late[c + 1])
+            d_quantize(c + 1)
             h_quantize(1, late[c], P)
-        own_bf[1, late[3]] = sb("tail_bf", [P, PACK * P], BF16, "head_bf")
+        own_bf[1, late[3]] = late_d[3]
         h_gain(1, late[3])
         h_quantize(1, late[3], P)
 

@@ -30,6 +30,7 @@ HALF = 512
 BANK = 512
 RUN = 32
 EIGHT = 8
+SHARE = 96
 GAIN_BANK = 7
 
 
@@ -57,8 +58,7 @@ def tile_list_unfollow_forecast_features_kernel(
 
         window_bytes = 2 * T
         third_piece = passes * window_bytes
-        first_sig = third_piece + 4 * KP
-        head_tanh = first_sig + 4 * PACK * HALF
+        head_tanh = third_piece + 4 * PACK * KP
 
         list1 = keep.tile([P, S // 16], U16, name="list1")
         list2 = keep.tile([P, S // 16], U16, name="list2")
@@ -275,10 +275,7 @@ def tile_list_unfollow_forecast_features_kernel(
 
         def d_first(f, indices):
             banks = [bank(index, [P, HALF]) for index in indices]
-            if f == 0:
-                sig = at("sig0", [P, PACK, HALF], F32, first_sig)
-            else:
-                sig = sb("sig1", [P, PACK, HALF], F32)
+            sig = sb("sig%d" % f, [P, PACK, HALF], F32)
             for t in range(PACK):
                 for a in range(passes):
                     nc.tensor.matmul_mx(
@@ -346,7 +343,7 @@ def tile_list_unfollow_forecast_features_kernel(
             h_tanh(early[c], 0, CH * c)
         h_first((6, 0), 0, 3 * CH, CH)
         third_bf = sb("third_bf", [P, PACK * KP], BF16)
-        nc.scalar.copy(dealt(third_bf[:]), rows_of(0, 1))
+        nc.scalar.copy(dealt(third_bf[:])[:, 0:SHARE], rows_of(0, 1)[:, 0:SHARE])
         sig = [d_first(0, (1, 2, 3, 4)), d_first(1, (5, 6, 0, 1))]
         for c in range(4):
             h_gain(0, CH * c)
@@ -355,6 +352,14 @@ def tile_list_unfollow_forecast_features_kernel(
         nc.gpsimd.tensor_scalar(
             last_bf[:].rearrange("p (t m j) -> p m t j", t=PACK, j=PACK),
             w1_raw[1, 1].rearrange("p j (m t) -> p m t j", t=PACK),
+            1.0,
+            0.0,
+            MULT,
+            ADD,
+        )
+        nc.gpsimd.tensor_scalar(
+            third_bf[:].rearrange("p (t m j) -> p m t j", t=PACK, j=PACK)[:, SHARE:P],
+            w1_raw[0, 1].rearrange("p j (m t) -> p m t j", t=PACK)[:, SHARE:P],
             1.0,
             0.0,
             MULT,

@@ -87,10 +87,9 @@ def tile_list_unfollow_forecast_features_kernel(
         nc.scalar.activation(warm_out[:], warm_in[:], ACT.Sigmoid)
 
         def load_scale_rows(plane, scales):
-            for q in range(QUADS):
+            for r in range(SROWS):
                 nc.sync.dma_start(
-                    plane[QUAD * q : QUAD * q + SROWS].bitcast(I32),
-                    scales[:, SROWS * q : SROWS * (q + 1), :].rearrange("a r c -> r a c").bitcast(I32),
+                    plane[r:P:QUAD].bitcast(I32), scales[:, r : QUADS * SROWS : SROWS, :].rearrange("a q c -> q a c").bitcast(I32)
                 )
 
         nc.gpsimd.memset(rows[:], 0.0)
@@ -112,10 +111,10 @@ def tile_list_unfollow_forecast_features_kernel(
             w1_raw[a, b] = raw
 
         def move_scales(a):
-            for q in range(QUADS):
-                row = LIVE + QUADS * SROWS * a + SROWS * q
+            first = LIVE + QUADS * SROWS * a
+            for r in range(SROWS):
                 nc.sync.dma_start(
-                    planes[a][QUAD * q : QUAD * q + SROWS].bitcast(I32), picked[row : row + SROWS].bitcast(I32)
+                    planes[a][r:P:QUAD].bitcast(I32), picked[first + r : first + QUADS * SROWS : SROWS].bitcast(I32)
                 )
 
         def quantize(name, values, tag=None, place=None):
@@ -150,9 +149,9 @@ def tile_list_unfollow_forecast_features_kernel(
         gather(picked[:, 0, :], swin, list1, 0, S)
         gather(picked[:, 1, :], swin, list2, 0, S)
         move_scales(0)
+        nc.sync.dma_start(w2_raw[:], w2_words.rearrange("a p c i -> p a (c i)").bitcast(I32))
         load_tab(1)
         load_scale_rows(w2s_raw, w2_scales)
-        nc.sync.dma_start(w2_raw[:], w2_words.rearrange("a p c i -> p a (c i)").bitcast(I32))
         move_scales(1)
         load_w1(1, 1)
         load_w1(0, 1)

from contextlib import ExitStack

import concourse.mybir as mybir
from concourse.masks import make_identity

K, T, S, H, G, N = 1024, 4096, 1024, 1024, 512, 512
FLOPS = 2 * S * (K * H + K * G + H * N + G * N)

F32 = mybir.dt.float32
BF16 = mybir.dt.bfloat16
I32 = mybir.dt.int32
U32 = mybir.dt.uint32
U16 = mybir.dt.uint16
U8 = mybir.dt.uint8
FP8X4 = mybir.dt.float8_e4m3fn_x4
FP4X4 = mybir.dt.float4_e2m1fn_x4
ACT = mybir.ActivationFunctionType
MULT = mybir.AluOpType.mult
ADD = mybir.AluOpType.add

P = 128
PACK = 4
KP = P * PACK
QUADS = 4
QUAD = 32
SROWS = 4
LIVE = 96
CH = 256
HALF = 512
BANK = 512
RUN = 32
EIGHT = 8
SHARE = 96
GAIN_BANK = 7


def tile_list_unfollow_forecast_features_kernel(
    tc, tab_words, tab_scales, offs, offs2, w1, gain1, w2_words, w2_scales, bias2, gain2, w3_words, w3_scales, w4, out
):
    nc = tc.nc
    passes = K // KP
    blocks = H // KP
    halves = S // HALF

    with ExitStack() as ctx:
        keep = ctx.enter_context(tc.tile_pool(name="keep", bufs=1))
        placed = ctx.enter_context(tc.tile_pool(name="placed", bufs=1))
        psum = ctx.enter_context(tc.psum_pool(name="psum", bufs=1))

        def sb(name, shape, dtype, tag=None):
            return keep.tile(shape, dtype, name=name, tag=tag or name, align_bytes=64)

        def at(name, shape, dtype, offset):
            return placed.tile(shape, dtype, name=name, align_bytes=64, offset=offset)

        def bank(index, shape):
            return psum.tile(shape, F32, name="bank%d" % index)

        window_bytes = 2 * T
        third_piece = passes * window_bytes
        head_tanh = third_piece + 4 * PACK * KP

        list1 = keep.tile([P, S // 16], U16, name="list1")
        list2 = keep.tile([P, S // 16], U16, name="list2")
        wwin = [at("wwin%d" % a, [P, T], U16, window_bytes * a) for a in range(passes)]
        swin = sb("swin", [P, T], U8)
        picked = sb("picked", [P, 2, S], U8)
        planes = [sb("plane%d" % a, [P, 2, S], U8) for a in range(passes)]
        g1 = sb("g1", [P, blocks, PACK], F32)
        rows = sb("rows", [P, P], F32)
        gain_bias = sb("gain_bias", [P, 2, PACK], F32)
        w2s_raw = sb("w2s_raw", [P, passes, G], U8)
        w3s = sb("w3s", [P, blocks, N], U8)
        w2_raw = sb("w2_raw", [P, passes, G], I32)
        w2c = sb("w2c", [P, PACK, passes, P], U32)
        w2s = sb("w2s", [P, PACK, passes, P], U8)
        w4_raw = sb("w4_raw", [P, PACK, N], F32)
        w3c = sb("w3c", [P, blocks, 2 * N], U8)
        ident = sb("ident", [P, P], F32)

        nc.vector.memset(swin[0:LIVE].bitcast(I32), 0)
        for a in range(passes):
            nc.vector.memset(planes[a][:].bitcast(I32), 0)
        warm_in = sb("warm_in", [P, 1], F32)
        warm_out = sb("warm_out", [P, 1], F32)
        nc.gpsimd.memset(warm_in[:], 0.0)
        nc.scalar.activation(warm_out[:], warm_in[:], ACT.Sigmoid)

        def load_scale_rows(plane, scales):
            for r in range(SROWS):
                nc.sync.dma_start(
                    plane[r:P:QUAD].bitcast(I32), scales[:, r : QUADS * SROWS : SROWS, :].rearrange("a q c -> q a c").bitcast(I32)
                )

        nc.gpsimd.memset(rows[:], 0.0)
        make_identity(nc, ident[:])
        nc.gpsimd.memset(w2s_raw[:].bitcast(I32), 0)
        nc.gpsimd.memset(w3s[:].bitcast(I32), 0)

        def load_tab(a):
            nc.sync.dma_start(wwin[a][:].bitcast(I32), tab_words[a].bitcast(I32))

        w1_raw = {}

        def load_w1(a, b):
            if (a, b) == (0, 1):
                raw = at("raw01", [P, PACK, KP], F32, third_piece)[:]
            else:
                raw = sb("raw%d%d" % (a, b), [P, PACK, KP], F32)[:]
            nc.sync.dma_start(raw, w1[KP * a : KP * (a + 1), KP * b : KP * (b + 1)].rearrange("(p j) c -> p j c", j=PACK))
            w1_raw[a, b] = raw

        def move_scales(a):
            first = LIVE + QUADS * SROWS * a
            for r in range(SROWS):
                nc.sync.dma_start(
                    planes[a][r:P:QUAD].bitcast(I32), picked[first + r : first + QUADS * SROWS : SROWS].bitcast(I32)
                )

        def quantize(name, values, tag=None, place=None):
            width = values.shape[1] // PACK
            codes = sb(name + "c", [P, width], U32)
            scales = sb(name + "s", [P, width], U8, tag) if place is None else at(name + "s", [P, width], U8, place)
            nc.vector.quantize_mx(out=codes[:].bitcast(FP8X4), scales=scales[:], in_=values)
            return codes, scales

        def dealt(grouped):
            return grouped.rearrange("p (t m j) -> p m j t", t=PACK, j=PACK)

        def rows_of(a, b):
            return w1_raw[a, b].rearrange("p j (m t) -> p m j t", t=PACK)

        def gather(dst, window, offsets, c0, c1):
            nc.vector.tensor_copy(dst, window[:].indirect(offsets[:, c0 // 16 : c1 // 16]))

        nc.sync.dma_start(list1[:], offs)
        nc.sync.dma_start(swin[LIVE:P].bitcast(I32), tab_scales.rearrange("a r c -> (a r) c").bitcast(I32))
        nc.sync.dma_start(list2[:], offs2)
        load_tab(0)
        nc.sync.dma_start(g1[:], gain1.rearrange("(b p t) -> p b t", b=blocks, t=PACK))
        for v, vector in enumerate((gain2, bias2)):
            nc.sync.dma_start(
                rows[PACK * v : PACK * (v + 1)].rearrange("t (b i) -> t b i", i=EIGHT),
                vector.rearrange("(b t i) -> t b i", t=PACK, i=EIGHT),
            )
        load_w1(0, 0)
        load_w1(1, 0)

        gather(picked[:, 0, :], swin, list1, 0, S)
        gather(picked[:, 1, :], swin, list2, 0, S)
        move_scales(0)
        nc.sync.dma_start(w2_raw[:], w2_words.rearrange("a p c i -> p a (c i)").bitcast(I32))
        load_tab(1)
        load_scale_rows(w2s_raw, w2_scales)
        move_scales(1)
        load_w1(1, 1)
        load_w1(0, 1)
        for t in range(PACK):
            nc.sync.dma_start(w4_raw[:, t, :], w4.rearrange("(b t i) n -> t b i n", t=PACK, i=EIGHT)[t])
        nc.sync.dma_start(w3c[:].bitcast(I32), w3_words.rearrange("a p n -> p a n").bitcast(I32))
        load_scale_rows(w3s, w3_scales)

        columns = bank(1, [P, P])
        nc.tensor.transpose(columns[:], rows[:], ident[:])
        nc.scalar.copy(gain_bias[:], columns[:, 0 : 2 * PACK].rearrange("p (v t) -> p v t", t=PACK))
        spread = sb("spread", [P, P], F32)
        nc.scalar.copy(
            spread[:, 0 : blocks * RUN].rearrange("p (b i t) -> p b i t", b=blocks, t=PACK),
            g1[:].rearrange("p b (i t) -> p b i t", i=1).to_broadcast([P, blocks, RUN // PACK, PACK]),
        )
        nc.scalar.copy(
            spread[:, blocks * RUN : P].rearrange("p (c t i) -> p c t i", t=PACK, i=PACK),
            columns[:, 0:PACK].rearrange("p (c t i) -> p c t i", c=1, i=1).to_broadcast([P, PACK, PACK, PACK]),
        )
        turned_ps = bank(0, [P, P])
        nc.tensor.transpose(turned_ps[:], spread[:], ident[:])
        turned = sb("turned", [P, P], F32)
        nc.scalar.copy(turned[:], turned_ps[:])
        gains = bank(GAIN_BANK, [P, P])
        nc.tensor.transpose(gains[:], turned[:], ident[:])

        v1 = [sb("v1_%d" % a, [P, S], U16) for a in range(passes)]
        v2 = [sb("v2_0", [P, S], U16, "raw00"), sb("v2_1", [P, S], U16)]

        w1_q = {}

        def early_w1(a):
            grouped = sb("w1bf%d" % a, [P, PACK * KP], BF16)
            nc.scalar.copy(dealt(grouped[:]), rows_of(a, 0))
            w1_q[a, 0] = quantize("w1q%d" % a, grouped[:]) + (0,)

        gather(v1[0][:], wwin[0], list1, 0, S)
        early_w1(0)
        gather(v2[0][:], wwin[0], list2, 0, S)
        early_w1(1)
        nc.scalar.copy(
            w2c[:].rearrange("p t a (b i) -> p t (a b) i", i=EIGHT),
            w2_raw[:].bitcast(U32).rearrange("p a (b t i) -> p t (a b) i", t=PACK, i=EIGHT),
        )
        nc.scalar.copy(
            w2s[:].bitcast(U32).rearrange("p t a (b i) -> p t (a b) i", i=2),
            w2s_raw[:].bitcast(U32).rearrange("p a (b t i) -> p t (a b) i", t=PACK, i=2),
        )
        for f in range(halves):
            gather(v1[1][:, HALF * f : HALF * (f + 1)], wwin[1], list1, HALF * f, HALF * (f + 1))
        gather(v2[1][:], wwin[1], list2, 0, S)

        line = sb("line", [P, PACK * (S + HALF)], BF16)
        own_bf = {(1, 0): sb("head_bf", [P, PACK * CH], BF16)[:]}
        h1_bf = sb("h1_bf", [P, PACK * S], BF16)

        def h_bf(b, c0, width):
            if (b, c0) in own_bf:
                return own_bf[b, c0]
            return (h1_bf if b == 1 else line)[:, PACK * c0 : PACK * (c0 + width)]

        def h_banks(indices, width):
            return [bank(index, [P, BANK // width, width]) for index in indices]

        def h_pass(banks, b, c0, a, tiles=range(PACK)):
            per, width = banks[0].shape[1:]
            codes, scales, first = w1_q[a, b]
            for t in tiles:
                cols = slice(first + P * t, first + P * (t + 1))
                nc.tensor.matmul_mx(
                    out=banks[t // per][:, t % per, :],
                    lhsT=codes[:, cols].bitcast(FP8X4),
                    lhsT_scale=scales[:, cols],
                    rhs=v1[a][:, c0 : c0 + width].bitcast(FP4X4),
                    rhs_scale=planes[a][:, 0, c0 : c0 + width],
                    start=(a == 0 and t % per == 0),
                    stop=(a == passes - 1 and t % per == per - 1),
                )

        th = {}

        def h_tanh(banks, b, c0):
            per, width = banks[0].shape[1:]
            if (b, c0) == (1, 0):
                th[b, c0] = at("th_head", [P, len(banks), width, per], F32, head_tanh)
            else:
                th[b, c0] = sb("th%d_%d" % (b, c0), [P, len(banks), width, per], F32)
            for u in range(len(banks)):
                nc.scalar.activation(th[b, c0][:, u], banks[u][:].rearrange("p e n -> p n e"), ACT.Tanh)

        def h_first(indices, b, c0, width):
            banks = h_banks(indices, width)
            per = BANK // width
            for u in range(len(banks)):
                for a in range(passes):
                    h_pass(banks, b, c0, a, range(per * u, per * (u + 1)))
            h_tanh(banks, b, c0)

        def h_gain(b, c0):
            regions, width, per = th[b, c0].shape[1:]
            entries = RUN // PACK
            nc.vector.tensor_tensor(
                h_bf(b, c0, width).rearrange("p (c i u e) -> p c i u e", i=entries, u=regions, e=per),
                th[b, c0][:].rearrange("p u (c i) e -> p c i u e", i=entries),
                gains[:, RUN * b : RUN * (b + 1)]
                .rearrange("p (c i u e) -> p c i u e", c=1, u=regions, e=per)
                .to_broadcast([P, width // entries, entries, regions, per]),
                MULT,
            )

        h_q = {}

        def h_quantize(b, c0, width, place=None):
            codes, scales = quantize("hq%d_%d" % (b, c0), h_bf(b, c0, width), None, place)
            for c in range(c0, c0 + width, P):
                h_q[b, c] = (codes, scales, c - c0)

        d_q = {}

        def d_first(f, indices):
            banks = [bank(index, [P, HALF]) for index in indices]
            sig = sb("sig%d" % f, [P, PACK, HALF], F32)
            for t in range(PACK):
                for a in range(passes):
                    nc.tensor.matmul_mx(
                        out=banks[t][:],
                        lhsT=w2c[:, t, a, :].bitcast(FP8X4),
                        lhsT_scale=w2s[:, t, a, :],
                        rhs=v2[a][:, HALF * f : HALF * (f + 1)].bitcast(FP4X4),
                        rhs_scale=planes[a][:, 1, HALF * f : HALF * (f + 1)],
                        start=(a == 0),
                        stop=(a == passes - 1),
                    )
                nc.scalar.activation(sig[:, t, :], banks[t][:], ACT.Sigmoid, bias=gain_bias[:, 1, t : t + 1])
            return sig

        def d_gain(dst, sig):
            nc.vector.tensor_tensor(
                dst.rearrange("p (c i t) -> p c t i", i=PACK, t=PACK),
                sig.rearrange("p t (c i) -> p c t i", i=PACK),
                gains[:, blocks * RUN : blocks * RUN + PACK * PACK]
                .rearrange("p (c t i) -> p c t i", c=1, i=PACK)
                .to_broadcast([P, sig.shape[2] // PACK, PACK, PACK]),
                MULT,
            )

        out_v = out.rearrange("(i p) j -> p i j", p=P)

        def y_passes(banks, c0, source, start=False, stop=False, tiles=range(N // P)):
            per, width = banks[0].shape[1:]
            codes, scales, first = d_q[c0] if source == "d" else h_q[source, c0]
            for i in tiles:
                cols = slice(P * i, P * (i + 1))
                if source == "d":
                    weights, weight_scales = d_q[0][0][:, cols].bitcast(FP8X4), d_q[0][1][:, cols]
                else:
                    weights, weight_scales = w3c[:, source, 2 * P * i : 2 * P * (i + 1)].bitcast(FP4X4), w3s[:, source, cols]
                nc.tensor.matmul_mx(
                    out=banks[i // per][:, i % per, :],
                    lhsT=weights,
                    lhsT_scale=weight_scales,
                    rhs=codes[:, first : first + width].bitcast(FP8X4),
                    rhs_scale=scales[:, first : first + width],
                    start=(start and i % per == 0),
                    stop=(stop and i % per == per - 1),
                )

        def y_open(indices, c0, width):
            banks = [bank(index, [P, N // P // len(indices), width]) for index in indices]
            y_passes(banks, c0, 0, start=True)
            return banks

        def y_close(banks, c0, sources):
            per, width = banks[0].shape[1:]
            for u in range(len(banks)):
                for source in sources:
                    y_passes(banks, c0, source, stop=(source == 1), tiles=range(per * u, per * (u + 1)))
                res = sb("res%d_%d" % (c0, u), [P, per, width], F32)
                nc.scalar.activation(res[:], banks[u][:], ACT.Gelu_apprx_tanh)
                nc.sync.dma_start(out_v[:, per * u : per * (u + 1), c0 : c0 + width], res[:])

        early = [h_banks((2 * c, 2 * c + 1), CH) for c in range(3)]
        for a in range(passes):
            for c in range(3):
                h_pass(early[c], 0, CH * c, a)
        for c in range(3):
            h_tanh(early[c], 0, CH * c)
        h_first((6, 0), 0, 3 * CH, CH)
        third_bf = sb("third_bf", [P, PACK * KP], BF16)
        nc.scalar.copy(dealt(third_bf[:])[:, 0:SHARE], rows_of(0, 1)[:, 0:SHARE])
        sig = [d_first(0, (1, 2, 3, 4)), d_first(1, (5, 6, 0, 1))]
        for c in range(4):
            h_gain(0, CH * c)

        last_bf = at("last_bf", [P, PACK * KP], BF16, window_bytes - PACK * KP)
        nc.gpsimd.tensor_scalar(
            last_bf[:].rearrange("p (t m j) -> p m t j", t=PACK, j=PACK),
            w1_raw[1, 1].rearrange("p j (m t) -> p m t j", t=PACK),
            1.0,
            0.0,
            MULT,
            ADD,
        )
        nc.gpsimd.tensor_scalar(
            third_bf[:].rearrange("p (t m j) -> p m t j", t=PACK, j=PACK)[:, SHARE:P],
            w1_raw[0, 1].rearrange("p j (m t) -> p m t j", t=PACK)[:, SHARE:P],
            1.0,
            0.0,
            MULT,
            ADD,
        )
        w1_q[1, 1] = quantize("w1q11", last_bf[:], None, third_piece) + (0,)
        w1_q[0, 1] = quantize("w1q01", third_bf[:]) + (0,)
        h_quantize(0, 0, S, third_piece + KP)
        d_gain(line[:, PACK * S : PACK * (S + HALF)], sig[0][:])
        d1_bf = sb("d1_bf", [P, PACK * CH], BF16)
        d_gain(d1_bf[:, 0 : PACK * CH], sig[1][:, :, 0:CH])
        nc.gpsimd.tensor_scalar(
            line[:, PACK * HALF : PACK * S].rearrange("p (c t) -> p c t", t=PACK),
            w4_raw[:].rearrange("p t c -> p c t"),
            1.0,
            0.0,
            MULT,
            ADD,
        )

        h_first((2, 3), 1, 0, CH)
        h_first((4, 5), 1, CH, CH)
        late = [HALF + P * c for c in range(4)]
        for c in range(4):
            h_first(((6 + c) % GAIN_BANK,), 1, late[c], P)

        h_gain(1, 0)
        d_q[0] = quantize("w4d", line[:, PACK * HALF : PACK * (S + HALF)]) + (N,)
        d_q[CH] = d_q[0][0:2] + (N + CH,)
        h_quantize(1, 0, CH)
        h_gain(1, CH)
        d_gain(line[:, PACK * S : PACK * (S + CH)], sig[1][:, :, CH:HALF])
        own_bf[1, late[0]] = sb("side_bf", [P, PACK * P], BF16, "head_bf")[:]
        nc.gpsimd.tensor_tensor(
            own_bf[1, late[0]].rearrange("p (n t) -> p n t", t=PACK),
            th[1, late[0]][:, 0],
            g1[:, 1:2, :].to_broadcast([P, P, PACK]),
            MULT,
        )
        late_d = [(d1_bf if c < 2 else line[:, PACK * S :])[:, PACK * P * (c % 2) : PACK * P * (c % 2 + 1)] for c in range(4)]

        def d_quantize(c):
            d_q[late[c]] = quantize("dq%d" % c, late_d[c], None, head_tanh + P * c) + (0,)

        d_quantize(0)
        h_quantize(1, CH, CH)
        h_quantize(1, late[0], P)
        d_quantize(1)
        for c in range(1, 3):
            h_gain(1, late[c])
            d_quantize(c + 1)
            h_quantize(1, late[c], P)
        own_bf[1, late[3]] = late_d[3]
        h_gain(1, late[3])
        h_quantize(1, late[3], P)

        first = y_open((1, 2), 0, CH)
        second = y_open((3, 4), CH, CH)
        y_passes(first, 0, "d")
        parts = [y_open(((5, 6, 0)[c],), late[c], P) for c in range(3)]
        y_close(first, 0, (1,))
        y_passes(second, CH, "d")
        y_close(second, CH, (1,))
        parts.append(y_open((1, 2), late[3], P))
        y_passes(parts[0], late[0], "d")
        for c in range(4):
            if c + 1 < 4:
                y_passes(parts[c + 1], late[c + 1], "d")
            y_close(parts[c], late[c], (1,))
